import numpy as np
import ml_dtypes


def mxq(x, axis, fmt="e4m3"):
    dtype, down = {"e4m3": (ml_dtypes.float8_e4m3fn, 7), "e5m2": (ml_dtypes.float8_e5m2, 14)}[fmt]
    v = np.moveaxis(np.asarray(x, np.float32).astype(ml_dtypes.bfloat16).astype(np.float64), axis, -1)
    blocks = v.reshape(v.shape[:-1] + (-1, 32))
    amax = np.abs(blocks).max(-1, keepdims=True)
    byte = np.maximum(np.where(amax > 0, np.frexp(amax)[1] - 1 + 127, 0) - down, 1)
    scale = np.exp2(byte - 127.0)
    codes = (blocks / scale).astype(np.float32).astype(dtype).astype(np.float64)
    return np.moveaxis((codes * scale).reshape(v.shape), -1, axis)


WIDE = False


def mx_kscale(k):
    if not WIDE:
        return np.ones(k)
    levels = np.array([10, -10, 5, -5, 0])
    if k % 512:
        return np.exp2(np.random.permutation(np.resize(levels, k // 32))).repeat(32)
    a = np.empty((k // 512, 16))
    for p in range(k // 512):
        a[p, :8] = np.random.permutation(np.resize(levels, 8))
        for g in range(8):
            far = levels[np.abs(levels - a[p, g]) >= 10]
            a[p, g + 8] = far[np.random.randint(len(far))]
    return np.exp2(a.ravel()).repeat(32)


def f64(x):
    return np.asarray(x).astype(np.float64)


def striped(idx):
    return np.tile(idx.reshape(-1, 16).T, (8, 1)).astype(np.uint16)


def unstriped(offs):
    return offs[:16].T.reshape(-1).astype(np.int64)


E2M1 = np.array([0.0, 0.5, 1.0, 1.5, 2.0, 3.0, 4.0, 6.0, -0.0, -0.5, -1.0, -1.5, -2.0, -3.0, -4.0, -6.0])


def pack_fp4(w):
    k, n = w.shape
    w = f64(np.asarray(w, np.float32).astype(ml_dtypes.bfloat16)).reshape(k // 32, 32, n)
    amax = np.abs(w).max(1)
    mant, ex = np.frexp(amax / 6.0)
    byte = np.clip(np.where(amax > 0, np.where(mant > 0.5, ex, ex - 1) + 127, 1), 1, 254)
    scaled = (w * np.exp2(127.0 - byte)[:, None, :]).reshape(k, n).astype(np.float32)
    c = np.ascontiguousarray(scaled.reshape(k // 512, 128, 4, n).transpose(0, 1, 3, 2)).astype(ml_dtypes.float4_e2m1fn).view(np.uint8) & 0xF
    words = (c[..., 0::2] | (c[..., 1::2] << 4)).reshape(k // 512, 128, 2 * n)
    return np.ascontiguousarray(words), np.ascontiguousarray(byte.astype(np.uint8).reshape(k // 512, 16, n))


def unpack_fp4(words, scales):
    g, _, n = scales.shape
    words = np.ascontiguousarray(words).reshape(g, 128, n, 2)
    nib = np.empty((g, 128, n, 4), np.uint8)
    nib[..., 0::2] = words & 0xF
    nib[..., 1::2] = words >> 4
    vals = E2M1[nib] * np.repeat(np.exp2(scales.astype(np.float64) - 127.0), 8, axis=1)[..., None]
    return vals.transpose(0, 1, 3, 2).reshape(g * 512, n)


def relu(v):
    return np.maximum(v, 0.0)


K, T, H, N = 512, 512, 512, 128


def setup_inputs():
    n = np.random.standard_normal
    s = mx_kscale(K)[:, None]
    u = mx_kscale(H)
    packed_xT = pack_fp4(n((K, T)) * s)
    return {
        "x_words": packed_xT[0],
        "x_scales": packed_xT[1],
        "w1": (n((K, H)) / np.sqrt(2 * K) / s * u).astype(np.float32),
        "w2": (n((K, H)) / np.sqrt(2 * K) / s * u).astype(np.float32),
        "w3": (n((H, N)) / np.sqrt(H) / u[:, None]).astype(np.float32),
        "pos1": striped(np.random.permutation(T)),
        "pos2": striped(np.random.permutation(T)),
        "pos3": striped(np.random.permutation(T)),
        "pos4": striped(np.random.permutation(T)),
    }


def reference(x_words, x_scales, w1, w2, w3, pos1, pos2, pos3, pos4):
    xq = unpack_fp4(x_words, x_scales)
    y = mxq(f64(w1), 0, "e4m3").T @ xq
    e = mxq(f64(w2), 0, "e4m3").T @ xq
    z = np.maximum(np.maximum(np.maximum(relu(y + e[:, unstriped(pos1)]), relu(y + e[:, unstriped(pos2)])), relu(y + e[:, unstriped(pos3)])), relu(y + e[:, unstriped(pos4)]))
    return mxq(f64(w3), 0, "e4m3").T @ mxq(z, 0, "e4m3")

@@ -1,0 +1,161 @@
+from contextlib import ExitStack
+
+import concourse.mybir as mybir
+
+K, T, H, N = 512, 512, 512, 128
+FLOPS = 2 * K * H * T * 2 + 2 * H * N * T
+
+F32 = mybir.dt.float32
+BF16 = mybir.dt.bfloat16
+I32 = mybir.dt.int32
+U32 = mybir.dt.uint32
+U16 = mybir.dt.uint16
+U8 = mybir.dt.uint8
+FP8X4 = mybir.dt.float8_e4m3fn_x4
+FP4X4 = mybir.dt.float4_e2m1fn_x4
+RELU = mybir.ActivationFunctionType.Relu
+ADD = mybir.AluOpType.add
+MAX = mybir.AluOpType.max
+
+P = 128
+PACK = 4
+WINDOW = T + 16
+LIST_ROWS = 16
+LAST_PIECES = ((0, 256), (256, 128), (384, 128))
+
+
+def tile_picked_wedgecv_relu_l_kernel(
+    tc, x_words, x_scales, w1, w2, w3, pos1, pos2, pos3, pos4, out
+):
+    nc = tc.nc
+    with ExitStack() as ctx:
+        lists = ctx.enter_context(tc.tile_pool(name="lists", bufs=1))
+        keep = ctx.enter_context(tc.tile_pool(name="keep", bufs=1))
+        ring = ctx.enter_context(tc.tile_pool(name="ring", bufs=2))
+        psum = ctx.enter_context(tc.psum_pool(name="psum", bufs=8))
+
+        x_codes = keep.tile([P, 2 * T], U8, name="x_codes", align_bytes=64)
+        x_plane = keep.tile([P, T], U8, name="x_plane", align_bytes=64)
+        nc.gpsimd.memset(x_plane[:].bitcast(I32), 0)
+        nc.sync.dma_start(x_codes[:].bitcast(I32), x_words[0].bitcast(I32))
+        for q in range(4):
+            nc.scalar.dma_start(
+                x_plane[32 * q : 32 * q + 4, :].bitcast(I32), x_scales[0, 4 * q : 4 * q + 4, :].bitcast(I32)
+            )
+
+        offsets = [lists.tile([P, T // LIST_ROWS], U16, name="offsets%d" % d) for d in range(4)]
+        nc.sync.dma_start(offsets[0][:], pos1)
+        w2_raw = keep.tile([P, PACK, H], F32, name="w2_raw")
+        nc.sync.dma_start(w2_raw[:], w2.rearrange("(p j) c -> p j c", j=PACK))
+        w1_raw = keep.tile([P, PACK, H], F32, name="w1_raw")
+        nc.sync.dma_start(w1_raw[:], w1.rearrange("(p j) c -> p j c", j=PACK))
+        for tile, pos in zip(offsets[1:], (pos2, pos3, pos4)):
+            nc.sync.dma_start(tile[:], pos)
+
+        w3_raw = keep.tile([P, PACK, N], F32, name="w3_raw")
+        nc.sync.dma_start(w3_raw[:], w3.rearrange("(p j) n -> p j n", j=PACK))
+
+        windows = [keep.tile([P, WINDOW], F32, name="window%d" % t) for t in range(PACK)]
+        for t in range(1, PACK):
+            nc.gpsimd.memset(windows[t][:, T:], 0.0)
+        nc.scalar.activation(windows[0][:, T:], windows[1][:, T:], RELU)
+
+        def deal(copy, raw, dealt, lo, hi):
+            copy(
+                dealt[:, lo:hi].rearrange("p t m j -> p m t j"),
+                raw[:].rearrange("p j (m t) -> p m t j", t=PACK)[:, :, lo:hi, :],
+            )
+
+        def quantize(dealt, codes, plane, lo, hi):
+            nc.vector.quantize_mx(
+                codes[:, lo * P : hi * P].bitcast(FP8X4),
+                plane[:, lo * P : hi * P],
+                dealt[:, lo:hi].rearrange("p t m j -> p (t m j)"),
+            )
+
+        w2_bf = keep.tile([P, PACK, P, PACK], BF16, name="w2_bf", align_bytes=64)
+        w2_codes = keep.tile([P, H], U32, name="w2_codes", align_bytes=64)
+        w2_plane = keep.tile([P, H], U8, name="w2_plane", align_bytes=64)
+        deal(nc.vector.tensor_copy, w2_raw, w2_bf, 0, 2)
+        deal(nc.scalar.copy, w2_raw, w2_bf, 2, 4)
+        quantize(w2_bf, w2_codes, w2_plane, 0, 2)
+        quantize(w2_bf, w2_codes, w2_plane, 2, 4)
+
+        w1_bf = keep.tile([P, PACK, P, PACK], BF16, name="w1_bf", align_bytes=64)
+        w1_codes = keep.tile([P, H], U32, name="w1_codes", align_bytes=64)
+        w1_plane = keep.tile([P, H], U8, name="w1_plane", align_bytes=64)
+        deal(nc.vector.tensor_copy, w1_raw, w1_bf, 0, 1)
+        quantize(w1_bf, w1_codes, w1_plane, 0, 1)
+        deal(nc.vector.tensor_copy, w1_raw, w1_bf, 1, 4)
+        quantize(w1_bf, w1_codes, w1_plane, 1, 2)
+        quantize(w1_bf, w1_codes, w1_plane, 2, 4)
+
+        def project(codes, plane, t, dst):
+            acc = psum.tile([P, T], F32, name="acc")
+            cols = slice(t * P, (t + 1) * P)
+            nc.tensor.matmul_mx(
+                acc[:], codes[:, cols].bitcast(FP8X4), plane[:, cols], x_codes[:].bitcast(FP4X4), x_plane[:],
+                start=True, stop=True,
+            )
+            nc.scalar.copy(dst, acc[:])
+
+        centre = []
+        for t in range(PACK):
+            project(w2_codes, w2_plane, t, windows[t][:, :T])
+            y_t = keep.tile([P, T], F32, name="centre%d" % t)
+            project(w1_codes, w1_plane, t, y_t[:])
+            centre.append(y_t)
+
+        w3_bf = keep.tile([P, N, PACK], BF16, name="w3_bf", align_bytes=64)
+        w3_codes = keep.tile([P, N], U32, name="w3_codes", align_bytes=64)
+        w3_plane = keep.tile([P, N], U8, name="w3_plane", align_bytes=64)
+
+        def gather(d, first, count, edges):
+            for t in range(PACK):
+                picked = windows[t][:].indirect(offsets[d][:, first // LIST_ROWS : (first + count) // LIST_ROWS])
+                nc.vector.tensor_tensor(edges[:, t, :], picked, centre[t][:, first : first + count], ADD)
+
+        def round_relu(edges, dst):
+            nc.scalar.activation(dst, edges[:].rearrange("p t v -> p v t"), RELU)
+
+        rounded = []
+        for d in range(3):
+            edges = ring.tile([P, PACK, T], F32, name="edges")
+            gather(d, 0, T, edges)
+            dst = keep.tile([P, T, PACK], BF16, name="rounded%d" % d)
+            round_relu(edges, dst[:])
+            rounded.append(dst)
+            if d == 0:
+                nc.scalar.copy(w3_bf[:], w3_raw[:].rearrange("p j n -> p n j"))
+                nc.vector.quantize_mx(w3_codes[:].bitcast(FP8X4), w3_plane[:], w3_bf[:].rearrange("p n j -> p (n j)"))
+        best01 = keep.tile([P, T, PACK], BF16, name="best01")
+        nc.vector.tensor_tensor(best01[:], rounded[0][:], rounded[1][:], MAX)
+        best012 = keep.tile([P, T, PACK], BF16, name="best012")
+
+        for i, (first, count) in enumerate(LAST_PIECES):
+            cols = slice(first, first + count)
+            if i == 0:
+                edges = ring.tile([P, PACK, count], F32, name="edges")
+            else:
+                edges = keep.tile([P, PACK, count], F32, name="edges_last%d" % i)
+            gather(3, first, count, edges)
+            if i == 0:
+                nc.vector.tensor_tensor(best012[:], best01[:], rounded[2][:], MAX)
+            z = keep.tile([P, count, PACK], BF16, name="z%d" % i, align_bytes=64)
+            if i < len(LAST_PIECES) - 1:
+                last = keep.tile([P, count, PACK], BF16, name="rounded_last%d" % i)
+                round_relu(edges, last[:])
+                nc.vector.tensor_tensor(z[:], best012[:, cols, :], last[:], MAX)
+            else:
+                nc.vector.tensor_tensor(z[:], best012[:, cols, :], edges[:].rearrange("p t v -> p v t"), MAX)
+            z_codes = keep.tile([P, count], U32, name="z_codes%d" % i, align_bytes=64)
+            z_plane = keep.tile([P, count], U8, name="z_plane%d" % i, align_bytes=64)
+            nc.vector.quantize_mx(z_codes[:].bitcast(FP8X4), z_plane[:], z[:].rearrange("p v t -> p (v t)"))
+            acc = psum.tile([P, count], F32, name="acc")
+            nc.tensor.matmul_mx(
+                acc[:], w3_codes[:].bitcast(FP8X4), w3_plane[:], z_codes[:].bitcast(FP8X4), z_plane[:],
+                start=True, stop=True,
+            )
+            result = keep.tile([P, count], F32, name="result%d" % i)
+            nc.scalar.copy(result[:], acc[:])
+            nc.sync.dma_start(out[:, cols], result[:])

@@ -31,39 +31,41 @@ def tile_picked_wedgecv_relu_l_kernel(
     with ExitStack() as ctx:
         lists = ctx.enter_context(tc.tile_pool(name="lists", bufs=1))
         keep = ctx.enter_context(tc.tile_pool(name="keep", bufs=1))
-        ring = ctx.enter_context(tc.tile_pool(name="ring", bufs=2))
-        psum = ctx.enter_context(tc.psum_pool(name="psum", bufs=8))
+        psum = ctx.enter_context(tc.psum_pool(name="psum", bufs=1))
 
         x_codes = keep.tile([P, 2 * T], U8, name="x_codes", align_bytes=64)
         x_plane = keep.tile([P, T], U8, name="x_plane", align_bytes=64)
-        nc.gpsimd.memset(x_plane[:].bitcast(I32), 0)
+        nc.vector.memset(x_plane[:].bitcast(I32), 0)
+
+        def load_halves(w, name):
+            halves = []
+            for half in range(2):
+                raw = keep.tile([P, PACK, H // 2], F32, name="%s_raw%d" % (name, half))
+                cols = slice(half * H // 2, (half + 1) * H // 2)
+                nc.sync.dma_start(raw[:], w[:, cols].rearrange("(p j) c -> p j c", j=PACK))
+                halves.append(raw)
+            return halves
+
+        w2_raw = load_halves(w2, "w2")
         nc.sync.dma_start(x_codes[:].bitcast(I32), x_words[0].bitcast(I32))
         for q in range(4):
-            nc.scalar.dma_start(
+            nc.sync.dma_start(
                 x_plane[32 * q : 32 * q + 4, :].bitcast(I32), x_scales[0, 4 * q : 4 * q + 4, :].bitcast(I32)
             )
-
+        w1_raw = load_halves(w1, "w1")
         offsets = [lists.tile([P, T // LIST_ROWS], U16, name="offsets%d" % d) for d in range(4)]
-        nc.sync.dma_start(offsets[0][:], pos1)
-        w2_raw = keep.tile([P, PACK, H], F32, name="w2_raw")
-        nc.sync.dma_start(w2_raw[:], w2.rearrange("(p j) c -> p j c", j=PACK))
-        w1_raw = keep.tile([P, PACK, H], F32, name="w1_raw")
-        nc.sync.dma_start(w1_raw[:], w1.rearrange("(p j) c -> p j c", j=PACK))
-        for tile, pos in zip(offsets[1:], (pos2, pos3, pos4)):
+        for tile, pos in zip(offsets, (pos1, pos2, pos3, pos4)):
             nc.sync.dma_start(tile[:], pos)
-
-        w3_raw = keep.tile([P, PACK, N], F32, name="w3_raw")
-        nc.sync.dma_start(w3_raw[:], w3.rearrange("(p j) n -> p j n", j=PACK))
 
         windows = [keep.tile([P, WINDOW], F32, name="window%d" % t) for t in range(PACK)]
         for t in range(1, PACK):
-            nc.gpsimd.memset(windows[t][:, T:], 0.0)
+            nc.vector.memset(windows[t][:, T:], 0.0)
         nc.scalar.activation(windows[0][:, T:], windows[1][:, T:], RELU)
 
-        def deal(copy, raw, dealt, lo, hi):
+        def deal(copy, raw, dealt, half, lo, hi):
             copy(
-                dealt[:, lo:hi].rearrange("p t m j -> p m t j"),
-                raw[:].rearrange("p j (m t) -> p m t j", t=PACK)[:, :, lo:hi, :],
+                dealt[:, lo:hi, half * P // 2 : (half + 1) * P // 2].rearrange("p t m j -> p m t j"),
+                raw[half][:].rearrange("p j (m t) -> p m t j", t=PACK)[:, :, lo:hi, :],
             )
 
         def quantize(dealt, codes, plane, lo, hi):
@@ -76,52 +78,74 @@ def tile_picked_wedgecv_relu_l_kernel(
         w2_bf = keep.tile([P, PACK, P, PACK], BF16, name="w2_bf", align_bytes=64)
         w2_codes = keep.tile([P, H], U32, name="w2_codes", align_bytes=64)
         w2_plane = keep.tile([P, H], U8, name="w2_plane", align_bytes=64)
-        deal(nc.vector.tensor_copy, w2_raw, w2_bf, 0, 2)
-        deal(nc.scalar.copy, w2_raw, w2_bf, 2, 4)
+        deal(nc.vector.tensor_copy, w2_raw, w2_bf, 0, 0, 4)
+        deal(nc.vector.tensor_copy, w2_raw, w2_bf, 1, 0, 2)
+        deal(nc.scalar.copy, w2_raw, w2_bf, 1, 2, 4)
         quantize(w2_bf, w2_codes, w2_plane, 0, 2)
         quantize(w2_bf, w2_codes, w2_plane, 2, 4)
 
-        w1_bf = keep.tile([P, PACK, P, PACK], BF16, name="w1_bf", align_bytes=64)
+        w1_bf = keep.tile([P, PACK, P, PACK], BF16, name="w1_bf", tag="w1_then_w3", align_bytes=64)
         w1_codes = keep.tile([P, H], U32, name="w1_codes", align_bytes=64)
         w1_plane = keep.tile([P, H], U8, name="w1_plane", align_bytes=64)
-        deal(nc.vector.tensor_copy, w1_raw, w1_bf, 0, 1)
+        deal(nc.vector.tensor_copy, w1_raw, w1_bf, 0, 0, 4)
+        deal(nc.vector.tensor_copy, w1_raw, w1_bf, 1, 0, 1)
+        deal(nc.vector.tensor_copy, w1_raw, w1_bf, 1, 1, 2)
+        deal(nc.scalar.copy, w1_raw, w1_bf, 1, 2, 4)
         quantize(w1_bf, w1_codes, w1_plane, 0, 1)
-        deal(nc.vector.tensor_copy, w1_raw, w1_bf, 1, 4)
         quantize(w1_bf, w1_codes, w1_plane, 1, 2)
         quantize(w1_bf, w1_codes, w1_plane, 2, 4)
 
-        def project(codes, plane, t, dst):
-            acc = psum.tile([P, T], F32, name="acc")
+        w3_raw = keep.tile([P, PACK, N], F32, name="w3_raw", tag="w1_then_w3", align_bytes=64)
+        nc.sync.dma_start(w3_raw[:], w3.rearrange("(p j) n -> p j n", j=PACK))
+
+        banks = [psum.tile([P, T], F32, name="bank%d" % b) for b in range(8)]
+
+        def project(codes, plane, t, bank, dst, first, count):
             cols = slice(t * P, (t + 1) * P)
             nc.tensor.matmul_mx(
-                acc[:], codes[:, cols].bitcast(FP8X4), plane[:, cols], x_codes[:].bitcast(FP4X4), x_plane[:],
-                start=True, stop=True,
+                bank[:, :count],
+                codes[:, cols].bitcast(FP8X4),
+                plane[:, cols],
+                x_codes[:, 2 * first : 2 * (first + count)].bitcast(FP4X4),
+                x_plane[:, first : first + count],
+                start=True,
+                stop=True,
             )
-            nc.scalar.copy(dst, acc[:])
+            nc.scalar.copy(dst[:, first : first + count], bank[:, :count])
 
-        centre = []
-        for t in range(PACK):
-            project(w2_codes, w2_plane, t, windows[t][:, :T])
-            y_t = keep.tile([P, T], F32, name="centre%d" % t)
-            project(w1_codes, w1_plane, t, y_t[:])
-            centre.append(y_t)
+        centre = [keep.tile([P, T], F32, name="centre%d" % t) for t in range(PACK)]
+        project(w2_codes, w2_plane, 0, banks[0], windows[0], 0, T)
+        project(w2_codes, w2_plane, 1, banks[1], windows[1], 0, T)
+        project(w1_codes, w1_plane, 0, banks[2], centre[0], 0, T // 2)
+        project(w1_codes, w1_plane, 0, banks[3], centre[0], T // 2, T // 2)
+        project(w1_codes, w1_plane, 1, banks[4], centre[1], 0, T)
+        project(w2_codes, w2_plane, 2, banks[5], windows[2], 0, T)
+        project(w1_codes, w1_plane, 2, banks[0], centre[2], 0, T)
+        project(w2_codes, w2_plane, 3, banks[3], windows[3], 0, T)
+        project(w1_codes, w1_plane, 3, banks[1], centre[3], 0, T)
 
         w3_bf = keep.tile([P, N, PACK], BF16, name="w3_bf", align_bytes=64)
         w3_codes = keep.tile([P, N], U32, name="w3_codes", align_bytes=64)
         w3_plane = keep.tile([P, N], U8, name="w3_plane", align_bytes=64)
 
-        def gather(d, first, count, edges):
-            for t in range(PACK):
-                picked = windows[t][:].indirect(offsets[d][:, first // LIST_ROWS : (first + count) // LIST_ROWS])
-                nc.vector.tensor_tensor(edges[:, t, :], picked, centre[t][:, first : first + count], ADD)
+        def gather(d, t, first, count, dst):
+            picked = windows[t][:].indirect(offsets[d][:, first // LIST_ROWS : (first + count) // LIST_ROWS])
+            nc.vector.tensor_tensor(dst, picked, centre[t][:, first : first + count], ADD)
 
         def round_relu(edges, dst):
-            nc.scalar.activation(dst, edges[:].rearrange("p t v -> p v t"), RELU)
+            nc.scalar.activation(
+                dst.rearrange("p (c i) t -> p c t i", i=4), edges[:].rearrange("p t (c i) -> p c t i", i=4), RELU
+            )
 
         rounded = []
         for d in range(3):
-            edges = ring.tile([P, PACK, T], F32, name="edges")
-            gather(d, 0, T, edges)
+            edges = keep.tile([P, PACK, T], F32, name="edges%d" % d)
+            for t in range(PACK):
+                if d == 0 and t == 0:
+                    gather(d, t, 0, T // 2, edges[:, t, : T // 2])
+                    gather(d, t, T // 2, T // 2, edges[:, t, T // 2 :])
+                else:
+                    gather(d, t, 0, T, edges[:, t, :])
             dst = keep.tile([P, T, PACK], BF16, name="rounded%d" % d)
             round_relu(edges, dst[:])
             rounded.append(dst)
@@ -134,14 +158,12 @@ def tile_picked_wedgecv_relu_l_kernel(
 
         for i, (first, count) in enumerate(LAST_PIECES):
             cols = slice(first, first + count)
-            if i == 0:
-                edges = ring.tile([P, PACK, count], F32, name="edges")
-            else:
-                edges = keep.tile([P, PACK, count], F32, name="edges_last%d" % i)
-            gather(3, first, count, edges)
+            edges = keep.tile([P, PACK, count], F32, name="edges_last%d" % i, tag="piece%d" % i, align_bytes=64)
+            for t in range(PACK):
+                gather(3, t, first, count, edges[:, t, :])
             if i == 0:
                 nc.vector.tensor_tensor(best012[:], best01[:], rounded[2][:], MAX)
-            z = keep.tile([P, count, PACK], BF16, name="z%d" % i, align_bytes=64)
+            z = keep.tile([P, count, PACK], BF16, name="z%d" % i, tag="piece%d" % (2 if i == 0 else 3 + i), align_bytes=64)
             if i < len(LAST_PIECES) - 1:
                 last = keep.tile([P, count, PACK], BF16, name="rounded_last%d" % i)
                 round_relu(edges, last[:])
@@ -151,11 +173,11 @@ def tile_picked_wedgecv_relu_l_kernel(
             z_codes = keep.tile([P, count], U32, name="z_codes%d" % i, align_bytes=64)
             z_plane = keep.tile([P, count], U8, name="z_plane%d" % i, align_bytes=64)
             nc.vector.quantize_mx(z_codes[:].bitcast(FP8X4), z_plane[:], z[:].rearrange("p v t -> p (v t)"))
-            acc = psum.tile([P, count], F32, name="acc")
+            acc = banks[(6, 7, 2)[i]][:, :count]
             nc.tensor.matmul_mx(
-                acc[:], w3_codes[:].bitcast(FP8X4), w3_plane[:], z_codes[:].bitcast(FP8X4), z_plane[:],
+                acc, w3_codes[:].bitcast(FP8X4), w3_plane[:], z_codes[:].bitcast(FP8X4), z_plane[:],
                 start=True, stop=True,
             )
             result = keep.tile([P, count], F32, name="result%d" % i)
-            nc.scalar.copy(result[:], acc[:])
-            nc.sync.dma_start(out[:, cols], result[:])
+            nc.scalar.copy(result[:], acc)
+            nc.scalar.dma_start(out[:, cols], result[:])

@@ -21,7 +21,8 @@ P = 128
 PACK = 4
 WINDOW = T + 16
 LIST_ROWS = 16
-LAST_PIECES = ((0, 256), (256, 128), (384, 128))
+LAST_PIECES = ((0, 256), (256, 192), (448, 64))
+PRODUCTS = (((0, 256),), ((256, 128), (384, 64)), ((448, 64),))
 
 
 def tile_picked_wedgecv_relu_l_kernel(
@@ -43,16 +44,18 @@ def tile_picked_wedgecv_relu_l_kernel(
                 raw = keep.tile([P, PACK, H // 2], F32, name="%s_raw%d" % (name, half))
                 cols = slice(half * H // 2, (half + 1) * H // 2)
                 nc.sync.dma_start(raw[:], w[:, cols].rearrange("(p j) c -> p j c", j=PACK))
-                halves.append(raw)
+                halves.append(raw[:])
             return halves
 
-        w2_raw = load_halves(w2, "w2")
-        nc.sync.dma_start(x_codes[:].bitcast(I32), x_words[0].bitcast(I32))
+        w2_whole = keep.tile([P, PACK, H], F32, name="w2_raw")
+        nc.sync.dma_start(w2_whole[:], w2.rearrange("(p j) c -> p j c", j=PACK))
+        w2_raw = [w2_whole[:, :, : H // 2], w2_whole[:, :, H // 2 :]]
         for q in range(4):
             nc.sync.dma_start(
                 x_plane[32 * q : 32 * q + 4, :].bitcast(I32), x_scales[0, 4 * q : 4 * q + 4, :].bitcast(I32)
             )
         w1_raw = load_halves(w1, "w1")
+        nc.sync.dma_start(x_codes[:].bitcast(I32), x_words[0].bitcast(I32))
         offsets = [lists.tile([P, T // LIST_ROWS], U16, name="offsets%d" % d) for d in range(4)]
         for tile, pos in zip(offsets, (pos1, pos2, pos3, pos4)):
             nc.sync.dma_start(tile[:], pos)
@@ -65,7 +68,7 @@ def tile_picked_wedgecv_relu_l_kernel(
         def deal(copy, raw, dealt, half, lo, hi):
             copy(
                 dealt[:, lo:hi, half * P // 2 : (half + 1) * P // 2].rearrange("p t m j -> p m t j"),
-                raw[half][:].rearrange("p j (m t) -> p m t j", t=PACK)[:, :, lo:hi, :],
+                raw[half].rearrange("p j (m t) -> p m t j", t=PACK)[:, :, lo:hi, :],
             )
 
         def quantize(dealt, codes, plane, lo, hi):
@@ -79,10 +82,8 @@ def tile_picked_wedgecv_relu_l_kernel(
         w2_codes = keep.tile([P, H], U32, name="w2_codes", align_bytes=64)
         w2_plane = keep.tile([P, H], U8, name="w2_plane", align_bytes=64)
         deal(nc.vector.tensor_copy, w2_raw, w2_bf, 0, 0, 4)
-        deal(nc.vector.tensor_copy, w2_raw, w2_bf, 1, 0, 2)
-        deal(nc.scalar.copy, w2_raw, w2_bf, 1, 2, 4)
-        quantize(w2_bf, w2_codes, w2_plane, 0, 2)
-        quantize(w2_bf, w2_codes, w2_plane, 2, 4)
+        deal(nc.scalar.copy, w2_raw, w2_bf, 1, 0, 4)
+        quantize(w2_bf, w2_codes, w2_plane, 0, 4)
 
         w1_bf = keep.tile([P, PACK, P, PACK], BF16, name="w1_bf", tag="w1_then_w3", align_bytes=64)
         w1_codes = keep.tile([P, H], U32, name="w1_codes", align_bytes=64)
@@ -114,14 +115,15 @@ def tile_picked_wedgecv_relu_l_kernel(
             nc.scalar.copy(dst[:, first : first + count], bank[:, :count])
 
         centre = [keep.tile([P, T], F32, name="centre%d" % t) for t in range(PACK)]
-        project(w2_codes, w2_plane, 0, banks[0], windows[0], 0, T)
-        project(w2_codes, w2_plane, 1, banks[1], windows[1], 0, T)
+        project(w2_codes, w2_plane, 0, banks[0], windows[0], 0, T // 2)
+        project(w2_codes, w2_plane, 0, banks[1], windows[0], T // 2, T // 2)
         project(w1_codes, w1_plane, 0, banks[2], centre[0], 0, T // 2)
         project(w1_codes, w1_plane, 0, banks[3], centre[0], T // 2, T // 2)
         project(w1_codes, w1_plane, 1, banks[4], centre[1], 0, T)
-        project(w2_codes, w2_plane, 2, banks[5], windows[2], 0, T)
+        project(w2_codes, w2_plane, 1, banks[2], windows[1], 0, T)
+        project(w2_codes, w2_plane, 2, banks[3], windows[2], 0, T)
         project(w1_codes, w1_plane, 2, banks[0], centre[2], 0, T)
-        project(w2_codes, w2_plane, 3, banks[3], windows[3], 0, T)
+        project(w2_codes, w2_plane, 3, banks[4], windows[3], 0, T)
         project(w1_codes, w1_plane, 3, banks[1], centre[3], 0, T)
 
         w3_bf = keep.tile([P, N, PACK], BF16, name="w3_bf", align_bytes=64)
@@ -139,7 +141,7 @@ def tile_picked_wedgecv_relu_l_kernel(
 
         rounded = []
         for d in range(3):
-            edges = keep.tile([P, PACK, T], F32, name="edges%d" % d)
+            edges = keep.tile([P, PACK, T], F32, name="edges%d" % d, tag="edges%d" % d, align_bytes=64)
             for t in range(PACK):
                 if d == 0 and t == 0:
                     gather(d, t, 0, T // 2, edges[:, t, : T // 2])
@@ -158,26 +160,31 @@ def tile_picked_wedgecv_relu_l_kernel(
 
         for i, (first, count) in enumerate(LAST_PIECES):
             cols = slice(first, first + count)
-            edges = keep.tile([P, PACK, count], F32, name="edges_last%d" % i, tag="piece%d" % i, align_bytes=64)
+            edges = keep.tile([P, PACK, count], F32, name="edges_last%d" % i, tag=("edges0", "edges1", "piece2")[i], align_bytes=64)
             for t in range(PACK):
                 gather(3, t, first, count, edges[:, t, :])
             if i == 0:
                 nc.vector.tensor_tensor(best012[:], best01[:], rounded[2][:], MAX)
-            z = keep.tile([P, count, PACK], BF16, name="z%d" % i, tag="piece%d" % (2 if i == 0 else 3 + i), align_bytes=64)
+            z = keep.tile([P, count, PACK], BF16, name="z%d" % i, align_bytes=64)
             if i < len(LAST_PIECES) - 1:
-                last = keep.tile([P, count, PACK], BF16, name="rounded_last%d" % i)
+                last = keep.tile(
+                    [P, count, PACK], BF16, name="rounded_last%d" % i, tag="piece%d" % (i + 1), align_bytes=64
+                )
                 round_relu(edges, last[:])
                 nc.vector.tensor_tensor(z[:], best012[:, cols, :], last[:], MAX)
             else:
                 nc.vector.tensor_tensor(z[:], best012[:, cols, :], edges[:].rearrange("p t v -> p v t"), MAX)
             z_codes = keep.tile([P, count], U32, name="z_codes%d" % i, align_bytes=64)
             z_plane = keep.tile([P, count], U8, name="z_plane%d" % i, align_bytes=64)
-            nc.vector.quantize_mx(z_codes[:].bitcast(FP8X4), z_plane[:], z[:].rearrange("p v t -> p (v t)"))
-            acc = banks[(6, 7, 2)[i]][:, :count]
-            nc.tensor.matmul_mx(
-                acc, w3_codes[:].bitcast(FP8X4), w3_plane[:], z_codes[:].bitcast(FP8X4), z_plane[:],
-                start=True, stop=True,
-            )
             result = keep.tile([P, count], F32, name="result%d" % i)
-            nc.scalar.copy(result[:], acc)
+            for start, width in PRODUCTS[i]:
+                own = slice(start - first, start - first + width)
+                nc.vector.quantize_mx(
+                    z_codes[:, own].bitcast(FP8X4), z_plane[:, own], z[:, own, :].rearrange("p v t -> p (v t)")
+                )
+                nc.tensor.matmul_mx(
+                    banks[5 + i][:, own], w3_codes[:].bitcast(FP8X4), w3_plane[:], z_codes[:, own].bitcast(FP8X4),
+                    z_plane[:, own], start=True, stop=True,
+                )
+            nc.scalar.copy(result[:], banks[5 + i][:, :count])
             nc.scalar.dma_start(out[:, cols], result[:])

@@ -38,23 +38,14 @@ def tile_picked_wedgecv_relu_l_kernel(
         x_plane = keep.tile([P, T], U8, name="x_plane", align_bytes=64)
         nc.vector.memset(x_plane[:].bitcast(I32), 0)
 
-        def load_halves(w, name):
-            halves = []
-            for half in range(2):
-                raw = keep.tile([P, PACK, H // 2], F32, name="%s_raw%d" % (name, half))
-                cols = slice(half * H // 2, (half + 1) * H // 2)
-                nc.sync.dma_start(raw[:], w[:, cols].rearrange("(p j) c -> p j c", j=PACK))
-                halves.append(raw[:])
-            return halves
-
-        w2_whole = keep.tile([P, PACK, H], F32, name="w2_raw")
-        nc.sync.dma_start(w2_whole[:], w2.rearrange("(p j) c -> p j c", j=PACK))
-        w2_raw = [w2_whole[:, :, : H // 2], w2_whole[:, :, H // 2 :]]
+        w2_raw = keep.tile([P, PACK, H], F32, name="w2_raw")
+        nc.sync.dma_start(w2_raw[:], w2.rearrange("(p j) c -> p j c", j=PACK))
         for q in range(4):
             nc.sync.dma_start(
                 x_plane[32 * q : 32 * q + 4, :].bitcast(I32), x_scales[0, 4 * q : 4 * q + 4, :].bitcast(I32)
             )
-        w1_raw = load_halves(w1, "w1")
+        w1_raw = keep.tile([P, PACK, H], F32, name="w1_raw")
+        nc.sync.dma_start(w1_raw[:], w1.rearrange("(p j) c -> p j c", j=PACK))
         nc.sync.dma_start(x_codes[:].bitcast(I32), x_words[0].bitcast(I32))
         offsets = [lists.tile([P, T // LIST_ROWS], U16, name="offsets%d" % d) for d in range(4)]
         for tile, pos in zip(offsets, (pos1, pos2, pos3, pos4)):
@@ -65,10 +56,10 @@ def tile_picked_wedgecv_relu_l_kernel(
             nc.vector.memset(windows[t][:, T:], 0.0)
         nc.scalar.activation(windows[0][:, T:], windows[1][:, T:], RELU)
 
-        def deal(copy, raw, dealt, half, lo, hi):
+        def deal(copy, raw, dealt, lo, hi):
             copy(
-                dealt[:, lo:hi, half * P // 2 : (half + 1) * P // 2].rearrange("p t m j -> p m t j"),
-                raw[half].rearrange("p j (m t) -> p m t j", t=PACK)[:, :, lo:hi, :],
+                dealt[:, lo:hi].rearrange("p t (q r) j -> p q t r j", r=8),
+                raw[:].rearrange("p j (q t r) -> p q t r j", t=PACK, r=8)[:, :, lo:hi],
             )
 
         def quantize(dealt, codes, plane, lo, hi):
@@ -81,23 +72,25 @@ def tile_picked_wedgecv_relu_l_kernel(
         w2_bf = keep.tile([P, PACK, P, PACK], BF16, name="w2_bf", align_bytes=64)
         w2_codes = keep.tile([P, H], U32, name="w2_codes", align_bytes=64)
         w2_plane = keep.tile([P, H], U8, name="w2_plane", align_bytes=64)
-        deal(nc.vector.tensor_copy, w2_raw, w2_bf, 0, 0, 4)
-        deal(nc.scalar.copy, w2_raw, w2_bf, 1, 0, 4)
+        deal(nc.vector.tensor_copy, w2_raw, w2_bf, 0, 4)
         quantize(w2_bf, w2_codes, w2_plane, 0, 4)
 
-        w1_bf = keep.tile([P, PACK, P, PACK], BF16, name="w1_bf", tag="w1_then_w3", align_bytes=64)
-        w1_codes = keep.tile([P, H], U32, name="w1_codes", align_bytes=64)
+        w1_bf = keep.tile([P, PACK, P, PACK], BF16, name="w1_bf", align_bytes=64)
+        w1_codes = keep.tile([P, H], U32, name="w1_codes", tag="w1_then_w3", align_bytes=64)
         w1_plane = keep.tile([P, H], U8, name="w1_plane", align_bytes=64)
-        deal(nc.vector.tensor_copy, w1_raw, w1_bf, 0, 0, 4)
-        deal(nc.vector.tensor_copy, w1_raw, w1_bf, 1, 0, 1)
-        deal(nc.vector.tensor_copy, w1_raw, w1_bf, 1, 1, 2)
-        deal(nc.scalar.copy, w1_raw, w1_bf, 1, 2, 4)
+        deal(nc.vector.tensor_copy, w1_raw, w1_bf, 0, 1)
+        deal(nc.vector.tensor_copy, w1_raw, w1_bf, 1, 2)
+        deal(nc.scalar.copy, w1_raw, w1_bf, 3, 4)
         quantize(w1_bf, w1_codes, w1_plane, 0, 1)
         quantize(w1_bf, w1_codes, w1_plane, 1, 2)
+        deal(nc.vector.tensor_copy, w1_raw, w1_bf, 2, 3)
         quantize(w1_bf, w1_codes, w1_plane, 2, 4)
 
-        w3_raw = keep.tile([P, PACK, N], F32, name="w3_raw", tag="w1_then_w3", align_bytes=64)
-        nc.sync.dma_start(w3_raw[:], w3.rearrange("(p j) n -> p j n", j=PACK))
+        w3_raw = keep.tile([P, PACK, N], F32, name="w3_raw")
+        for q in range(H // 32):
+            nc.sync.dma_start(
+                w3_raw[8 * q : 8 * q + 8], w3[32 * q : 32 * q + 32].rearrange("(t r) n -> r t n", t=PACK)
+            )
 
         banks = [psum.tile([P, T], F32, name="bank%d" % b) for b in range(8)]
 
@@ -126,7 +119,7 @@ def tile_picked_wedgecv_relu_l_kernel(
         project(w2_codes, w2_plane, 3, banks[4], windows[3], 0, T)
         project(w1_codes, w1_plane, 3, banks[1], centre[3], 0, T)
 
-        w3_bf = keep.tile([P, N, PACK], BF16, name="w3_bf", align_bytes=64)
+        w3_bf = keep.tile([P, N, PACK], BF16, name="w3_bf", tag="w1_then_w3", align_bytes=64)
         w3_codes = keep.tile([P, N], U32, name="w3_codes", align_bytes=64)
         w3_plane = keep.tile([P, N], U8, name="w3_plane", align_bytes=64)
 

@@ -1,6 +1,7 @@
 from contextlib import ExitStack
 
 import concourse.mybir as mybir
+from concourse.masks import make_identity
 
 K, T, H, N = 512, 512, 512, 128
 FLOPS = 2 * K * H * T * 2 + 2 * H * N * T
@@ -19,10 +20,10 @@ MAX = mybir.AluOpType.max
 
 P = 128
 PACK = 4
-WINDOW = T + 16
+WINDOW = 704
 LIST_ROWS = 16
-LAST_PIECES = ((0, 256), (256, 192), (448, 64))
-PRODUCTS = (((0, 256),), ((256, 128), (384, 64)), ((448, 64),))
+HALF = T // 2
+PIECES = ((0, 256), (256, 128), (384, 64), (448, 64))
 
 
 def tile_picked_wedgecv_relu_l_kernel(
@@ -44,140 +45,180 @@ def tile_picked_wedgecv_relu_l_kernel(
             nc.sync.dma_start(
                 x_plane[32 * q : 32 * q + 4, :].bitcast(I32), x_scales[0, 4 * q : 4 * q + 4, :].bitcast(I32)
             )
-        w1_raw = keep.tile([P, PACK, H], F32, name="w1_raw")
-        nc.sync.dma_start(w1_raw[:], w1.rearrange("(p j) c -> p j c", j=PACK))
         nc.sync.dma_start(x_codes[:].bitcast(I32), x_words[0].bitcast(I32))
         offsets = [lists.tile([P, T // LIST_ROWS], U16, name="offsets%d" % d) for d in range(4)]
-        for tile, pos in zip(offsets, (pos1, pos2, pos3, pos4)):
+        nc.sync.dma_start(offsets[0][:], pos1)
+        w1_raw = keep.tile([P, PACK, H], F32, name="w1_raw")
+        nc.sync.dma_start(w1_raw[:], w1.rearrange("(p j) c -> p j c", j=PACK))
+        for tile, pos in zip(offsets[1:], (pos2, pos3, pos4)):
             nc.sync.dma_start(tile[:], pos)
-
-        windows = [keep.tile([P, WINDOW], F32, name="window%d" % t) for t in range(PACK)]
-        for t in range(1, PACK):
-            nc.vector.memset(windows[t][:, T:], 0.0)
-        nc.scalar.activation(windows[0][:, T:], windows[1][:, T:], RELU)
-
-        def deal(copy, raw, dealt, lo, hi):
-            copy(
-                dealt[:, lo:hi].rearrange("p t (q r) j -> p q t r j", r=8),
-                raw[:].rearrange("p j (q t r) -> p q t r j", t=PACK, r=8)[:, :, lo:hi],
-            )
-
-        def quantize(dealt, codes, plane, lo, hi):
-            nc.vector.quantize_mx(
-                codes[:, lo * P : hi * P].bitcast(FP8X4),
-                plane[:, lo * P : hi * P],
-                dealt[:, lo:hi].rearrange("p t m j -> p (t m j)"),
-            )
-
-        w2_bf = keep.tile([P, PACK, P, PACK], BF16, name="w2_bf", align_bytes=64)
-        w2_codes = keep.tile([P, H], U32, name="w2_codes", align_bytes=64)
-        w2_plane = keep.tile([P, H], U8, name="w2_plane", align_bytes=64)
-        deal(nc.vector.tensor_copy, w2_raw, w2_bf, 0, 4)
-        quantize(w2_bf, w2_codes, w2_plane, 0, 4)
-
-        w1_bf = keep.tile([P, PACK, P, PACK], BF16, name="w1_bf", align_bytes=64)
-        w1_codes = keep.tile([P, H], U32, name="w1_codes", tag="w1_then_w3", align_bytes=64)
-        w1_plane = keep.tile([P, H], U8, name="w1_plane", align_bytes=64)
-        deal(nc.vector.tensor_copy, w1_raw, w1_bf, 0, 1)
-        deal(nc.vector.tensor_copy, w1_raw, w1_bf, 1, 2)
-        deal(nc.scalar.copy, w1_raw, w1_bf, 3, 4)
-        quantize(w1_bf, w1_codes, w1_plane, 0, 1)
-        quantize(w1_bf, w1_codes, w1_plane, 1, 2)
-        deal(nc.vector.tensor_copy, w1_raw, w1_bf, 2, 3)
-        quantize(w1_bf, w1_codes, w1_plane, 2, 4)
-
         w3_raw = keep.tile([P, PACK, N], F32, name="w3_raw")
         for q in range(H // 32):
             nc.sync.dma_start(
                 w3_raw[8 * q : 8 * q + 8], w3[32 * q : 32 * q + 32].rearrange("(t r) n -> r t n", t=PACK)
             )
 
+        windows = [keep.tile([P, WINDOW], F32, name="window%d" % t) for t in range(PACK)]
+        for t in range(1, PACK):
+            nc.vector.memset(windows[t][:, T:], 0.0)
+        nc.scalar.activation(windows[0][:, T:], windows[1][:, T:], RELU)
+        identity = keep.tile([P, P], F32, name="identity")
+        make_identity(nc, identity[:])
+
+        def deal(copy, raw, dealt, lo, hi, blocks=slice(0, 16)):
+            copy(
+                dealt.rearrange("p (t q r) j -> p q t r j", t=hi - lo, r=8)[:, blocks],
+                raw[:].rearrange("p j (q t r) -> p q t r j", t=PACK, r=8)[:, blocks, lo:hi],
+            )
+
+        def quantize(dealt, codes, plane):
+            nc.vector.quantize_mx(codes.bitcast(FP8X4), plane, dealt.rearrange("p m j -> p (m j)"))
+
+        def mx_tiles(name, layers):
+            return (
+                keep.tile([P, layers * P, PACK], BF16, name=name + "_bf", tag=name + "_bf", align_bytes=64),
+                keep.tile([P, layers * P], U32, name=name + "_codes", align_bytes=64),
+                keep.tile([P, layers * P], U8, name=name + "_plane", align_bytes=64),
+            )
+
+        def quantize_tiles(tiles):
+            quantize(tiles[0][:], tiles[1][:], tiles[2][:])
+
         banks = [psum.tile([P, T], F32, name="bank%d" % b) for b in range(8)]
 
-        def project(codes, plane, t, bank, dst, first, count):
-            cols = slice(t * P, (t + 1) * P)
+        def project(tiles, layer, bank, first, count):
+            cols = slice(layer * P, (layer + 1) * P)
             nc.tensor.matmul_mx(
                 bank[:, :count],
-                codes[:, cols].bitcast(FP8X4),
-                plane[:, cols],
+                tiles[1][:, cols].bitcast(FP8X4),
+                tiles[2][:, cols],
                 x_codes[:, 2 * first : 2 * (first + count)].bitcast(FP4X4),
                 x_plane[:, first : first + count],
                 start=True,
                 stop=True,
             )
-            nc.scalar.copy(dst[:, first : first + count], bank[:, :count])
 
+        w2_0, w2_12, w2_3 = mx_tiles("w2_0", 1), mx_tiles("w2_12", 2), mx_tiles("w2_3", 1)
+        deal(nc.vector.tensor_copy, w2_raw, w2_0[0][:], 0, 1, slice(0, 8))
+        deal(nc.scalar.copy, w2_raw, w2_0[0][:], 0, 1, slice(8, 16))
+        quantize_tiles(w2_0)
+        deal(nc.vector.tensor_copy, w2_raw, w2_12[0][:], 1, 3)
+        deal(nc.scalar.copy, w2_raw, w2_3[0][:], 3, 4)
+        quantize_tiles(w2_12)
+        quantize_tiles(w2_3)
+        for h in range(2):
+            project(w2_0, 0, banks[h], h * HALF, HALF)
+            nc.scalar.copy(windows[0][:, h * HALF : (h + 1) * HALF], banks[h][:, :HALF])
+        project(w2_12, 0, banks[4], 0, T)
+        project(w2_12, 1, banks[5], 0, T)
+        project(w2_3, 0, banks[6], 0, T)
+
+        w1_0, w1_1, w1_23 = mx_tiles("w1_0", 1), mx_tiles("w1_1", 1), mx_tiles("w1_23", 2)
         centre = [keep.tile([P, T], F32, name="centre%d" % t) for t in range(PACK)]
-        project(w2_codes, w2_plane, 0, banks[0], windows[0], 0, T // 2)
-        project(w2_codes, w2_plane, 0, banks[1], windows[0], T // 2, T // 2)
-        project(w1_codes, w1_plane, 0, banks[2], centre[0], 0, T // 2)
-        project(w1_codes, w1_plane, 0, banks[3], centre[0], T // 2, T // 2)
-        project(w1_codes, w1_plane, 1, banks[4], centre[1], 0, T)
-        project(w2_codes, w2_plane, 1, banks[2], windows[1], 0, T)
-        project(w2_codes, w2_plane, 2, banks[3], windows[2], 0, T)
-        project(w1_codes, w1_plane, 2, banks[0], centre[2], 0, T)
-        project(w2_codes, w2_plane, 3, banks[4], windows[3], 0, T)
-        project(w1_codes, w1_plane, 3, banks[1], centre[3], 0, T)
+        centre_banks = (banks[7], banks[2], banks[3], banks[0])
+        first_list = []
 
-        w3_bf = keep.tile([P, N, PACK], BF16, name="w3_bf", tag="w1_then_w3", align_bytes=64)
-        w3_codes = keep.tile([P, N], U32, name="w3_codes", align_bytes=64)
-        w3_plane = keep.tile([P, N], U8, name="w3_plane", align_bytes=64)
+        def gather_plain(t, tag):
+            first_list.append(keep.tile([P, T], F32, name="first_list%d" % t, tag=tag, align_bytes=64))
+            nc.vector.tensor_copy(first_list[t][:], windows[t][:].indirect(offsets[0][:]))
 
-        def gather(d, t, first, count, dst):
-            picked = windows[t][:].indirect(offsets[d][:, first // LIST_ROWS : (first + count) // LIST_ROWS])
-            nc.vector.tensor_tensor(dst, picked, centre[t][:, first : first + count], ADD)
+        gather_plain(0, "first_list0")
+        nc.scalar.copy(windows[1][:, :T], banks[4][:])
+        gather_plain(1, "first_list1")
+        deal(nc.scalar.copy, w1_raw, w1_0[0][:], 0, 1)
+        quantize_tiles(w1_0)
+        project(w1_0, 0, centre_banks[0], 0, T)
+        nc.scalar.copy(windows[2][:, :T], banks[5][:])
+        gather_plain(2, "w1_0_bf")
+        deal(nc.scalar.copy, w1_raw, w1_1[0][:], 1, 2)
+        quantize_tiles(w1_1)
+        project(w1_1, 0, centre_banks[1], 0, T)
+        nc.scalar.copy(windows[3][:, :T], banks[6][:])
+        gather_plain(3, "w1_1_bf")
+        deal(nc.scalar.copy, w1_raw, w1_23[0][:], 2, 4)
+        quantize_tiles(w1_23)
+        project(w1_23, 0, centre_banks[2], 0, T)
+        project(w1_23, 1, centre_banks[3], 0, T)
+        for t in range(PACK):
+            nc.scalar.copy(centre[t][:], centre_banks[t][:])
 
-        def round_relu(edges, dst):
+        def gather(d):
+            edges = keep.tile([P, PACK, T], F32, name="edges%d" % d)
+            for t in range(PACK):
+                nc.vector.tensor_tensor(edges[:, t, :], windows[t][:].indirect(offsets[d][:]), centre[t][:], ADD)
+            return edges
+
+        def round_relu(edges, dst, cols):
             nc.scalar.activation(
-                dst.rearrange("p (c i) t -> p c t i", i=4), edges[:].rearrange("p t (c i) -> p c t i", i=4), RELU
+                dst[:, cols, :].rearrange("p (c i) t -> p c t i", i=4),
+                edges[:, :, cols].rearrange("p t (c i) -> p c t i", i=4),
+                RELU,
             )
 
-        rounded = []
-        for d in range(3):
-            edges = keep.tile([P, PACK, T], F32, name="edges%d" % d, tag="edges%d" % d, align_bytes=64)
-            for t in range(PACK):
-                if d == 0 and t == 0:
-                    gather(d, t, 0, T // 2, edges[:, t, : T // 2])
-                    gather(d, t, T // 2, T // 2, edges[:, t, T // 2 :])
-                else:
-                    gather(d, t, 0, T, edges[:, t, :])
-            dst = keep.tile([P, T, PACK], BF16, name="rounded%d" % d)
-            round_relu(edges, dst[:])
-            rounded.append(dst)
-            if d == 0:
-                nc.scalar.copy(w3_bf[:], w3_raw[:].rearrange("p j n -> p n j"))
-                nc.vector.quantize_mx(w3_codes[:].bitcast(FP8X4), w3_plane[:], w3_bf[:].rearrange("p n j -> p (n j)"))
+        rounded = [keep.tile([P, T, PACK], BF16, name="rounded%d" % d) for d in range(3)]
+        edges1 = gather(1)
+
+        back_banks = (banks[7], banks[2])
+        for u in range(2):
+            for h in range(2):
+                bank = (banks[1], banks[4], banks[5], banks[6])[2 * u + h]
+                for b in range(2):
+                    cols = slice((2 * h + b) * P, (2 * h + b + 1) * P)
+                    for e in range(2):
+                        dst = bank[:, (2 * b + e) * P : (2 * b + e + 1) * P]
+                        t = 2 * u + e
+                        nc.tensor.matmul(
+                            dst, first_list[t][:, cols], identity[:], start=True, stop=False, is_transpose=True
+                        )
+                        nc.tensor.matmul(
+                            dst, centre[t][:, cols], identity[:], start=False, stop=True, is_transpose=True
+                        )
+                pairs = keep.tile([P, 2, P, 2], BF16, name="pairs%d%d" % (u, h))
+                nc.scalar.copy(pairs[:], bank[:].rearrange("v (b e p) -> v b p e", b=2, e=2))
+                words = pairs[:].rearrange("v b p e -> v (b p e)").bitcast(F32)
+                for b in range(2):
+                    nc.tensor.transpose(
+                        back_banks[h][:, (2 * u + b) * P : (2 * u + b + 1) * P],
+                        words[:, b * P : (b + 1) * P],
+                        identity[:],
+                    )
+        for h in range(2):
+            nc.scalar.copy(
+                rounded[0][:, h * HALF : (h + 1) * HALF, :].bitcast(F32),
+                back_banks[h][:].rearrange("p (u v) -> p v u", u=2),
+            )
+        round_relu(edges1, rounded[1], slice(0, T))
+
+        w3_bf = keep.tile([P, N, PACK], BF16, name="w3_bf", align_bytes=64)
+        w3_codes = keep.tile([P, N], U32, name="w3_codes", align_bytes=64)
+        w3_plane = keep.tile([P, N], U8, name="w3_plane", align_bytes=64)
+        nc.scalar.copy(w3_bf[:], w3_raw[:].rearrange("p j n -> p n j"))
+        quantize(w3_bf[:], w3_codes[:], w3_plane[:])
+
+        edges2 = gather(2)
+        round_relu(edges2, rounded[2], slice(0, T))
+        edges3 = gather(3)
         best01 = keep.tile([P, T, PACK], BF16, name="best01")
         nc.vector.tensor_tensor(best01[:], rounded[0][:], rounded[1][:], MAX)
         best012 = keep.tile([P, T, PACK], BF16, name="best012")
+        nc.vector.tensor_tensor(best012[:], best01[:], rounded[2][:], MAX)
 
-        for i, (first, count) in enumerate(LAST_PIECES):
+        last = keep.tile([P, T, PACK], BF16, name="rounded3")
+        out_banks = (banks[3], banks[0], banks[1], banks[4])
+        for i, (first, count) in enumerate(PIECES):
             cols = slice(first, first + count)
-            edges = keep.tile([P, PACK, count], F32, name="edges_last%d" % i, tag=("edges0", "edges1", "piece2")[i], align_bytes=64)
-            for t in range(PACK):
-                gather(3, t, first, count, edges[:, t, :])
-            if i == 0:
-                nc.vector.tensor_tensor(best012[:], best01[:], rounded[2][:], MAX)
+            round_relu(edges3, last, cols)
+        for i, (first, count) in enumerate(PIECES):
+            cols = slice(first, first + count)
             z = keep.tile([P, count, PACK], BF16, name="z%d" % i, align_bytes=64)
-            if i < len(LAST_PIECES) - 1:
-                last = keep.tile(
-                    [P, count, PACK], BF16, name="rounded_last%d" % i, tag="piece%d" % (i + 1), align_bytes=64
-                )
-                round_relu(edges, last[:])
-                nc.vector.tensor_tensor(z[:], best012[:, cols, :], last[:], MAX)
-            else:
-                nc.vector.tensor_tensor(z[:], best012[:, cols, :], edges[:].rearrange("p t v -> p v t"), MAX)
+            nc.vector.tensor_tensor(z[:], best012[:, cols, :], last[:, cols, :], MAX)
             z_codes = keep.tile([P, count], U32, name="z_codes%d" % i, align_bytes=64)
             z_plane = keep.tile([P, count], U8, name="z_plane%d" % i, align_bytes=64)
             result = keep.tile([P, count], F32, name="result%d" % i)
-            for start, width in PRODUCTS[i]:
-                own = slice(start - first, start - first + width)
-                nc.vector.quantize_mx(
-                    z_codes[:, own].bitcast(FP8X4), z_plane[:, own], z[:, own, :].rearrange("p v t -> p (v t)")
-                )
-                nc.tensor.matmul_mx(
-                    banks[5 + i][:, own], w3_codes[:].bitcast(FP8X4), w3_plane[:], z_codes[:, own].bitcast(FP8X4),
-                    z_plane[:, own], start=True, stop=True,
-                )
-            nc.scalar.copy(result[:], banks[5 + i][:, :count])
+            quantize(z[:], z_codes[:], z_plane[:])
+            nc.tensor.matmul_mx(
+                out_banks[i][:, :count], w3_codes[:].bitcast(FP8X4), w3_plane[:], z_codes[:].bitcast(FP8X4),
+                z_plane[:], start=True, stop=True,
+            )
+            nc.scalar.copy(result[:], out_banks[i][:, :count])
             nc.scalar.dma_start(out[:, cols], result[:])

@@ -23,7 +23,6 @@ PACK = 4
 WINDOW = 704
 LIST_ROWS = 16
 HALF = T // 2
-PIECES = ((0, 256), (256, 128), (384, 64), (448, 64))
 
 
 def tile_picked_wedgecv_relu_l_kernel(
@@ -113,7 +112,7 @@ def tile_picked_wedgecv_relu_l_kernel(
         project(w2_12, 1, banks[5], 0, T)
         project(w2_3, 0, banks[6], 0, T)
 
-        w1_0, w1_1, w1_23 = mx_tiles("w1_0", 1), mx_tiles("w1_1", 1), mx_tiles("w1_23", 2)
+        w1_01, w1_23 = mx_tiles("w1_01", 2), mx_tiles("w1_23", 2)
         centre = [keep.tile([P, T], F32, name="centre%d" % t) for t in range(PACK)]
         centre_banks = (banks[7], banks[2], banks[3], banks[0])
         first_list = []
@@ -125,16 +124,14 @@ def tile_picked_wedgecv_relu_l_kernel(
         gather_plain(0, "first_list0")
         nc.scalar.copy(windows[1][:, :T], banks[4][:])
         gather_plain(1, "first_list1")
-        deal(nc.scalar.copy, w1_raw, w1_0[0][:], 0, 1)
-        quantize_tiles(w1_0)
-        project(w1_0, 0, centre_banks[0], 0, T)
         nc.scalar.copy(windows[2][:, :T], banks[5][:])
-        gather_plain(2, "w1_0_bf")
-        deal(nc.scalar.copy, w1_raw, w1_1[0][:], 1, 2)
-        quantize_tiles(w1_1)
-        project(w1_1, 0, centre_banks[1], 0, T)
+        gather_plain(2, "first_list2")
+        deal(nc.scalar.copy, w1_raw, w1_01[0][:], 0, 2)
+        quantize_tiles(w1_01)
+        project(w1_01, 0, centre_banks[0], 0, T)
+        project(w1_01, 1, centre_banks[1], 0, T)
         nc.scalar.copy(windows[3][:, :T], banks[6][:])
-        gather_plain(3, "w1_1_bf")
+        gather_plain(3, "w1_01_bf")
         deal(nc.scalar.copy, w1_raw, w1_23[0][:], 2, 4)
         quantize_tiles(w1_23)
         project(w1_23, 0, centre_banks[2], 0, T)
@@ -143,7 +140,7 @@ def tile_picked_wedgecv_relu_l_kernel(
             nc.scalar.copy(centre[t][:], centre_banks[t][:])
 
         def gather(d):
-            edges = keep.tile([P, PACK, T], F32, name="edges%d" % d)
+            edges = keep.tile([P, PACK, T], F32, name="edges%d" % d, tag="edges%d" % d, align_bytes=64)
             for t in range(PACK):
                 nc.vector.tensor_tensor(edges[:, t, :], windows[t][:].indirect(offsets[d][:]), centre[t][:], ADD)
             return edges
@@ -198,27 +195,38 @@ def tile_picked_wedgecv_relu_l_kernel(
         edges2 = gather(2)
         round_relu(edges2, rounded[2], slice(0, T))
         edges3 = gather(3)
-        best01 = keep.tile([P, T, PACK], BF16, name="best01")
-        nc.vector.tensor_tensor(best01[:], rounded[0][:], rounded[1][:], MAX)
-        best012 = keep.tile([P, T, PACK], BF16, name="best012")
-        nc.vector.tensor_tensor(best012[:], best01[:], rounded[2][:], MAX)
-
+        halves = (slice(0, HALF), slice(HALF, T))
         last = keep.tile([P, T, PACK], BF16, name="rounded3")
-        out_banks = (banks[3], banks[0], banks[1], banks[4])
-        for i, (first, count) in enumerate(PIECES):
-            cols = slice(first, first + count)
+        for cols in halves:
             round_relu(edges3, last, cols)
-        for i, (first, count) in enumerate(PIECES):
-            cols = slice(first, first + count)
-            z = keep.tile([P, count, PACK], BF16, name="z%d" % i, align_bytes=64)
-            nc.vector.tensor_tensor(z[:], best012[:, cols, :], last[:, cols, :], MAX)
-            z_codes = keep.tile([P, count], U32, name="z_codes%d" % i, align_bytes=64)
-            z_plane = keep.tile([P, count], U8, name="z_plane%d" % i, align_bytes=64)
-            result = keep.tile([P, count], F32, name="result%d" % i)
-            quantize(z[:], z_codes[:], z_plane[:])
+        best01 = keep.tile([P, T, PACK], BF16, name="best01")
+        best012 = keep.tile([P, T, PACK], BF16, name="best012")
+        z = keep.tile([P, T, PACK], BF16, name="z", align_bytes=64)
+        for dst, a, b in ((best01, rounded[0], rounded[1]), (best012, best01, rounded[2]), (z, best012, last)):
+            for cols in halves:
+                nc.vector.tensor_tensor(dst[:, cols, :], a[:, cols, :], b[:, cols, :], MAX)
+
+        def project_out(bank, codes, plane, cols, copy, store):
+            count = cols.stop - cols.start
+            result = keep.tile([P, count], F32, name="result%d" % cols.start)
             nc.tensor.matmul_mx(
-                out_banks[i][:, :count], w3_codes[:].bitcast(FP8X4), w3_plane[:], z_codes[:].bitcast(FP8X4),
-                z_plane[:], start=True, stop=True,
+                bank[:, :count], w3_codes[:].bitcast(FP8X4), w3_plane[:], codes.bitcast(FP8X4), plane,
+                start=True, stop=True,
             )
-            nc.scalar.copy(result[:], out_banks[i][:, :count])
-            nc.scalar.dma_start(out[:, cols], result[:])
+            copy(result[:], bank[:, :count])
+            store(out[:, cols], result[:])
+
+        z_mx = []
+        for h, cols in enumerate(halves):
+            z_codes = keep.tile([P, HALF], U32, name="z_codes%d" % h, tag=("edges3", "z_codes1")[h], align_bytes=64)
+            z_plane = keep.tile([P, HALF], U8, name="z_plane%d" % h, align_bytes=64)
+            quantize(z[:, cols, :], z_codes[:], z_plane[:])
+            z_mx.append((z_codes, z_plane))
+        project_out(banks[3], z_mx[0][0][:], z_mx[0][1][:], halves[0], nc.scalar.copy, nc.scalar.dma_start)
+        project_out(
+            banks[0], z_mx[1][0][:, :P], z_mx[1][1][:, :P], slice(HALF, HALF + P),
+            nc.vector.tensor_copy, nc.sync.dma_start,
+        )
+        project_out(
+            banks[1], z_mx[1][0][:, P:], z_mx[1][1][:, P:], slice(HALF + P, T), nc.scalar.copy, nc.scalar.dma_start
+        )

@@ -75,13 +75,13 @@ def tile_picked_wedgecv_relu_l_kernel(
 
         def mx_tiles(name, layers):
             return (
-                keep.tile([P, layers * P, PACK], BF16, name=name + "_bf", tag=name + "_bf", align_bytes=64),
+                keep.tile([P, layers * P, PACK], BF16, name=name + "_bf", align_bytes=64)[:],
                 keep.tile([P, layers * P], U32, name=name + "_codes", align_bytes=64),
                 keep.tile([P, layers * P], U8, name=name + "_plane", align_bytes=64),
             )
 
         def quantize_tiles(tiles):
-            quantize(tiles[0][:], tiles[1][:], tiles[2][:])
+            quantize(tiles[0], tiles[1][:], tiles[2][:])
 
         banks = [psum.tile([P, T], F32, name="bank%d" % b) for b in range(8)]
 
@@ -97,52 +97,68 @@ def tile_picked_wedgecv_relu_l_kernel(
                 stop=True,
             )
 
-        w2_0, w2_12, w2_3 = mx_tiles("w2_0", 1), mx_tiles("w2_12", 2), mx_tiles("w2_3", 1)
-        deal(nc.vector.tensor_copy, w2_raw, w2_0[0][:], 0, 1, slice(0, 8))
-        deal(nc.scalar.copy, w2_raw, w2_0[0][:], 0, 1, slice(8, 16))
+        w2_0, w2_1, w2_23 = mx_tiles("w2_0", 1), mx_tiles("w2_1", 1), mx_tiles("w2_23", 2)
+        deal(nc.vector.tensor_copy, w2_raw, w2_0[0], 0, 1, slice(0, 10))
+        deal(nc.scalar.copy, w2_raw, w2_0[0], 0, 1, slice(10, 16))
         quantize_tiles(w2_0)
-        deal(nc.vector.tensor_copy, w2_raw, w2_12[0][:], 1, 3)
-        deal(nc.scalar.copy, w2_raw, w2_3[0][:], 3, 4)
-        quantize_tiles(w2_12)
-        quantize_tiles(w2_3)
-        for h in range(2):
-            project(w2_0, 0, banks[h], h * HALF, HALF)
-            nc.scalar.copy(windows[0][:, h * HALF : (h + 1) * HALF], banks[h][:, :HALF])
-        project(w2_12, 0, banks[4], 0, T)
-        project(w2_12, 1, banks[5], 0, T)
-        project(w2_3, 0, banks[6], 0, T)
+        deal(nc.scalar.copy, w2_raw, w2_1[0], 1, 2)
+        deal(nc.vector.tensor_copy, w2_raw, w2_23[0], 2, 4)
+        quantize_tiles(w2_1)
+        quantize_tiles(w2_23)
+        for bank, first, count in ((banks[0], 0, P), (banks[1], P, P), (banks[2], HALF, HALF)):
+            project(w2_0, 0, bank, first, count)
+            nc.scalar.copy(windows[0][:, first : first + count], bank[:, :count])
+        project(w2_1, 0, banks[4], 0, T)
+        project(w2_23, 0, banks[5], 0, T)
+        project(w2_23, 1, banks[6], 0, T)
 
-        w1_01, w1_23 = mx_tiles("w1_01", 2), mx_tiles("w1_23", 2)
+        picked_first = keep.tile([P, PACK * T + HALF], F32, name="picked_first", align_bytes=64)
+        first_list = [picked_first[:, t * T : (t + 1) * T] for t in range(PACK)]
+        w1_01_bf = picked_first[:, PACK * T - HALF :].bitcast(BF16).rearrange("p (m j) -> p m j", j=PACK)
+        w1_01 = (
+            w1_01_bf,
+            keep.tile([P, 2 * P], U32, name="w1_01_codes", align_bytes=64),
+            keep.tile([P, 2 * P], U8, name="w1_01_plane", align_bytes=64),
+        )
+        w1_23 = mx_tiles("w1_23", 2)
         centre = [keep.tile([P, T], F32, name="centre%d" % t) for t in range(PACK)]
-        centre_banks = (banks[7], banks[2], banks[3], banks[0])
-        first_list = []
+        centre_banks = (banks[7], banks[1], banks[3], banks[0])
 
-        def gather_plain(t, tag):
-            first_list.append(keep.tile([P, T], F32, name="first_list%d" % t, tag=tag, align_bytes=64))
-            nc.vector.tensor_copy(first_list[t][:], windows[t][:].indirect(offsets[0][:]))
+        def gather_plain(t):
+            nc.vector.tensor_copy(first_list[t], windows[t][:].indirect(offsets[0][:]))
 
-        gather_plain(0, "first_list0")
+        gather_plain(0)
         nc.scalar.copy(windows[1][:, :T], banks[4][:])
-        gather_plain(1, "first_list1")
+        gather_plain(1)
         nc.scalar.copy(windows[2][:, :T], banks[5][:])
-        gather_plain(2, "first_list2")
-        deal(nc.scalar.copy, w1_raw, w1_01[0][:], 0, 2)
-        quantize_tiles(w1_01)
-        project(w1_01, 0, centre_banks[0], 0, T)
+        gather_plain(2)
+        deal(nc.scalar.copy, w1_raw, w1_01[0], 0, 2)
+        for t in range(2):
+            cols = slice(t * P, (t + 1) * P)
+            quantize(w1_01[0][:, cols, :], w1_01[1][:, cols], w1_01[2][:, cols])
+        for bank, first in ((banks[7], 0), (banks[2], HALF)):
+            project(w1_01, 0, bank, first, HALF)
+            nc.scalar.copy(centre[0][:, first : first + HALF], bank[:, :HALF])
         project(w1_01, 1, centre_banks[1], 0, T)
         nc.scalar.copy(windows[3][:, :T], banks[6][:])
-        gather_plain(3, "w1_01_bf")
-        deal(nc.scalar.copy, w1_raw, w1_23[0][:], 2, 4)
+        gather_plain(3)
+        deal(nc.scalar.copy, w1_raw, w1_23[0], 2, 4)
         quantize_tiles(w1_23)
         project(w1_23, 0, centre_banks[2], 0, T)
         project(w1_23, 1, centre_banks[3], 0, T)
-        for t in range(PACK):
+        for t in range(1, PACK):
             nc.scalar.copy(centre[t][:], centre_banks[t][:])
+
+        halves = (slice(0, HALF), slice(HALF, T))
 
         def gather(d):
             edges = keep.tile([P, PACK, T], F32, name="edges%d" % d, tag="edges%d" % d, align_bytes=64)
-            for t in range(PACK):
-                nc.vector.tensor_tensor(edges[:, t, :], windows[t][:].indirect(offsets[d][:]), centre[t][:], ADD)
+            steps = [(t, slice(0, T)) for t in range(PACK)]
+            if d == 1:
+                steps[0:1] = [(0, cols) for cols in halves]
+            for t, cols in steps:
+                picked = windows[t][:].indirect(offsets[d][:, cols.start // LIST_ROWS : cols.stop // LIST_ROWS])
+                nc.vector.tensor_tensor(edges[:, t, cols], picked, centre[t][:, cols], ADD)
             return edges
 
         def round_relu(edges, dst, cols):
@@ -155,10 +171,10 @@ def tile_picked_wedgecv_relu_l_kernel(
         rounded = [keep.tile([P, T, PACK], BF16, name="rounded%d" % d) for d in range(3)]
         edges1 = gather(1)
 
-        back_banks = (banks[7], banks[2])
+        back_banks = (banks[7], banks[1])
         for u in range(2):
             for h in range(2):
-                bank = (banks[1], banks[4], banks[5], banks[6])[2 * u + h]
+                bank = (banks[2], banks[4], banks[5], banks[6])[2 * u + h]
                 for b in range(2):
                     cols = slice((2 * h + b) * P, (2 * h + b + 1) * P)
                     for e in range(2):
@@ -195,38 +211,43 @@ def tile_picked_wedgecv_relu_l_kernel(
         edges2 = gather(2)
         round_relu(edges2, rounded[2], slice(0, T))
         edges3 = gather(3)
-        halves = (slice(0, HALF), slice(HALF, T))
         last = keep.tile([P, T, PACK], BF16, name="rounded3")
         for cols in halves:
             round_relu(edges3, last, cols)
         best01 = keep.tile([P, T, PACK], BF16, name="best01")
         best012 = keep.tile([P, T, PACK], BF16, name="best012")
         z = keep.tile([P, T, PACK], BF16, name="z", align_bytes=64)
-        for dst, a, b in ((best01, rounded[0], rounded[1]), (best012, best01, rounded[2]), (z, best012, last)):
+        for dst, a, b in ((best01, rounded[0], rounded[1]), (best012, best01, rounded[2])):
             for cols in halves:
                 nc.vector.tensor_tensor(dst[:, cols, :], a[:, cols, :], b[:, cols, :], MAX)
 
-        def project_out(bank, codes, plane, cols, copy, store):
+        pieces = (slice(0, HALF), slice(HALF, HALF + P), slice(HALF + P, T))
+        out_banks = (banks[3], banks[0], banks[2])
+        copies = (nc.scalar.copy, nc.vector.tensor_copy, nc.scalar.copy)
+        stores = (nc.scalar.dma_start, nc.sync.dma_start, nc.scalar.dma_start)
+
+        def best_of_all(i):
+            cols = pieces[i]
+            nc.vector.tensor_tensor(z[:, cols, :], best012[:, cols, :], last[:, cols, :], MAX)
+
+        def project_out(i):
+            cols = pieces[i]
             count = cols.stop - cols.start
-            result = keep.tile([P, count], F32, name="result%d" % cols.start)
+            tag = "edges3" if i == 0 else "z_codes%d" % i
+            codes = keep.tile([P, count], U32, name="z_codes%d" % i, tag=tag, align_bytes=64)
+            plane = keep.tile([P, count], U8, name="z_plane%d" % i, align_bytes=64)
+            result = keep.tile([P, count], F32, name="result%d" % i)
+            quantize(z[:, cols, :], codes[:], plane[:])
             nc.tensor.matmul_mx(
-                bank[:, :count], w3_codes[:].bitcast(FP8X4), w3_plane[:], codes.bitcast(FP8X4), plane,
+                out_banks[i][:, :count], w3_codes[:].bitcast(FP8X4), w3_plane[:], codes[:].bitcast(FP8X4), plane[:],
                 start=True, stop=True,
             )
-            copy(result[:], bank[:, :count])
-            store(out[:, cols], result[:])
+            copies[i](result[:], out_banks[i][:, :count])
+            stores[i](out[:, cols], result[:])
 
-        z_mx = []
-        for h, cols in enumerate(halves):
-            z_codes = keep.tile([P, HALF], U32, name="z_codes%d" % h, tag=("edges3", "z_codes1")[h], align_bytes=64)
-            z_plane = keep.tile([P, HALF], U8, name="z_plane%d" % h, align_bytes=64)
-            quantize(z[:, cols, :], z_codes[:], z_plane[:])
-            z_mx.append((z_codes, z_plane))
-        project_out(banks[3], z_mx[0][0][:], z_mx[0][1][:], halves[0], nc.scalar.copy, nc.scalar.dma_start)
-        project_out(
-            banks[0], z_mx[1][0][:, :P], z_mx[1][1][:, :P], slice(HALF, HALF + P),
-            nc.vector.tensor_copy, nc.sync.dma_start,
-        )
-        project_out(
-            banks[1], z_mx[1][0][:, P:], z_mx[1][1][:, P:], slice(HALF + P, T), nc.scalar.copy, nc.scalar.dma_start
-        )
+        best_of_all(0)
+        best_of_all(1)
+        project_out(0)
+        best_of_all(2)
+        project_out(1)
+        project_out(2)

@@ -15,6 +15,7 @@ U8 = mybir.dt.uint8
 FP8X4 = mybir.dt.float8_e4m3fn_x4
 FP4X4 = mybir.dt.float4_e2m1fn_x4
 RELU = mybir.ActivationFunctionType.Relu
+MULT = mybir.AluOpType.mult
 ADD = mybir.AluOpType.add
 MAX = mybir.AluOpType.max
 
@@ -77,7 +78,7 @@ def tile_picked_wedgecv_relu_l_kernel(
             return (
                 keep.tile([P, layers * P, PACK], BF16, name=name + "_bf", align_bytes=64)[:],
                 keep.tile([P, layers * P], U32, name=name + "_codes", align_bytes=64),
-                keep.tile([P, layers * P], U8, name=name + "_plane", align_bytes=64),
+                keep.tile([P, layers * P], U8, name=name + "_plane", tag=name + "_plane", align_bytes=64),
             )
 
         def quantize_tiles(tiles):
@@ -115,12 +116,14 @@ def tile_picked_wedgecv_relu_l_kernel(
         picked_first = keep.tile([P, PACK * T + HALF], F32, name="picked_first", align_bytes=64)
         first_list = [picked_first[:, t * T : (t + 1) * T] for t in range(PACK)]
         w1_01_bf = picked_first[:, PACK * T - HALF :].bitcast(BF16).rearrange("p (m j) -> p m j", j=PACK)
-        w1_01 = (
-            w1_01_bf,
-            keep.tile([P, 2 * P], U32, name="w1_01_codes", align_bytes=64),
-            keep.tile([P, 2 * P], U8, name="w1_01_plane", align_bytes=64),
-        )
-        w1_23 = mx_tiles("w1_23", 2)
+        w1_0, w1_1 = [
+            (
+                w1_01_bf[:, t * P : (t + 1) * P, :],
+                keep.tile([P, P], U32, name="w1_%d_codes" % t, align_bytes=64),
+                keep.tile([P, P], U8, name="w1_%d_plane" % t, tag="w1_%d_plane" % t, align_bytes=64),
+            )
+            for t in range(2)
+        ]
         centre = [keep.tile([P, T], F32, name="centre%d" % t) for t in range(PACK)]
         centre_banks = (banks[7], banks[1], banks[3], banks[0])
 
@@ -132,17 +135,26 @@ def tile_picked_wedgecv_relu_l_kernel(
         gather_plain(1)
         nc.scalar.copy(windows[2][:, :T], banks[5][:])
         gather_plain(2)
-        deal(nc.scalar.copy, w1_raw, w1_01[0], 0, 2)
-        for t in range(2):
-            cols = slice(t * P, (t + 1) * P)
-            quantize(w1_01[0][:, cols, :], w1_01[1][:, cols], w1_01[2][:, cols])
+        deal(nc.scalar.copy, w1_raw, w1_01_bf, 0, 2)
+        quantize_tiles(w1_0)
+        quantize_tiles(w1_1)
         for bank, first in ((banks[7], 0), (banks[2], HALF)):
-            project(w1_01, 0, bank, first, HALF)
+            project(w1_0, 0, bank, first, HALF)
             nc.scalar.copy(centre[0][:, first : first + HALF], bank[:, :HALF])
-        project(w1_01, 1, centre_banks[1], 0, T)
+        project(w1_1, 0, centre_banks[1], 0, T)
         nc.scalar.copy(windows[3][:, :T], banks[6][:])
         gather_plain(3)
-        deal(nc.scalar.copy, w1_raw, w1_23[0], 2, 4)
+        w1_23 = (
+            keep.tile([P, 2 * P, PACK], BF16, name="w1_23_bf", align_bytes=64)[:],
+            keep.tile([P, 2 * P], U32, name="w1_23_codes", tag="w1_23_codes", align_bytes=64),
+            keep.tile([P, 2 * P], U8, name="w1_23_plane", tag="w1_0_plane", align_bytes=64),
+        )
+        for t in range(2):
+            nc.gpsimd.tensor_scalar(
+                w1_23[0][:, t * P : (t + 1) * P, :].rearrange("p (q r) j -> p q r j", r=8),
+                w1_raw[:].rearrange("p j (q t r) -> p t q r j", t=PACK, r=8)[:, 2 + t],
+                1.0, 0.0, MULT, ADD,
+            )
         quantize_tiles(w1_23)
         project(w1_23, 0, centre_banks[2], 0, T)
         project(w1_23, 1, centre_banks[3], 0, T)
@@ -202,7 +214,7 @@ def tile_picked_wedgecv_relu_l_kernel(
             )
         round_relu(edges1, rounded[1], slice(0, T))
 
-        w3_bf = keep.tile([P, N, PACK], BF16, name="w3_bf", align_bytes=64)
+        w3_bf = keep.tile([P, N, PACK], BF16, name="w3_bf", tag="w1_23_codes", align_bytes=64)
         w3_codes = keep.tile([P, N], U32, name="w3_codes", align_bytes=64)
         w3_plane = keep.tile([P, N], U8, name="w3_plane", align_bytes=64)
         nc.scalar.copy(w3_bf[:], w3_raw[:].rearrange("p j n -> p n j"))

@@ -18,10 +18,11 @@ RELU = mybir.ActivationFunctionType.Relu
 MULT = mybir.AluOpType.mult
 ADD = mybir.AluOpType.add
 MAX = mybir.AluOpType.max
+SUB = mybir.AluOpType.subtract
 
 P = 128
 PACK = 4
-WINDOW = 704
+WINDOW = 1024
 LIST_ROWS = 16
 HALF = T // 2
 
@@ -113,65 +114,63 @@ def tile_picked_wedgecv_relu_l_kernel(
         project(w2_23, 0, banks[5], 0, T)
         project(w2_23, 1, banks[6], 0, T)
 
-        picked_first = keep.tile([P, PACK * T + HALF], F32, name="picked_first", align_bytes=64)
-        first_list = [picked_first[:, t * T : (t + 1) * T] for t in range(PACK)]
-        w1_01_bf = picked_first[:, PACK * T - HALF :].bitcast(BF16).rearrange("p (m j) -> p m j", j=PACK)
-        w1_0, w1_1 = [
-            (
-                w1_01_bf[:, t * P : (t + 1) * P, :],
-                keep.tile([P, P], U32, name="w1_%d_codes" % t, align_bytes=64),
-                keep.tile([P, P], U8, name="w1_%d_plane" % t, tag="w1_%d_plane" % t, align_bytes=64),
-            )
-            for t in range(2)
-        ]
-        centre = [keep.tile([P, T], F32, name="centre%d" % t) for t in range(PACK)]
-        centre_banks = (banks[7], banks[1], banks[3], banks[0])
+        first_list = [keep.tile([P, T], F32, name="first_list%d" % t) for t in range(PACK)]
+        for t in range(PACK):
+            if t > 0:
+                nc.scalar.copy(windows[t][:, :T], banks[3 + t][:])
+            nc.vector.tensor_copy(first_list[t][:], windows[t][:].indirect(offsets[0][:]))
 
-        def gather_plain(t):
-            nc.vector.tensor_copy(first_list[t], windows[t][:].indirect(offsets[0][:]))
+        sum_banks = (banks[3], banks[7], banks[0], banks[1])
 
-        gather_plain(0)
-        nc.scalar.copy(windows[1][:, :T], banks[4][:])
-        gather_plain(1)
-        nc.scalar.copy(windows[2][:, :T], banks[5][:])
-        gather_plain(2)
-        deal(nc.scalar.copy, w1_raw, w1_01_bf, 0, 2)
-        quantize_tiles(w1_0)
-        quantize_tiles(w1_1)
-        for bank, first in ((banks[7], 0), (banks[2], HALF)):
-            project(w1_0, 0, bank, first, HALF)
-            nc.scalar.copy(centre[0][:, first : first + HALF], bank[:, :HALF])
-        project(w1_1, 0, centre_banks[1], 0, T)
-        nc.scalar.copy(windows[3][:, :T], banks[6][:])
-        gather_plain(3)
-        w1_23 = (
-            keep.tile([P, 2 * P, PACK], BF16, name="w1_23_bf", align_bytes=64)[:],
-            keep.tile([P, 2 * P], U32, name="w1_23_codes", tag="w1_23_codes", align_bytes=64),
-            keep.tile([P, 2 * P], U8, name="w1_23_plane", tag="w1_0_plane", align_bytes=64),
-        )
-        for t in range(2):
+        def turn(src, t, start, stop):
+            u, e = divmod(t, 2)
+            for h in range(2):
+                for b in range(2):
+                    nc.tensor.matmul(
+                        sum_banks[2 * u + h][:, (2 * b + e) * P : (2 * b + e + 1) * P],
+                        src[:, (2 * h + b) * P : (2 * h + b + 1) * P],
+                        identity[:],
+                        start=start and e == 0 and b == 0,
+                        stop=stop and e == 1 and b == 1,
+                        is_transpose=True,
+                    )
+
+        for t in range(PACK):
+            turn(first_list[t], t, True, False)
+
+        w1_all = mx_tiles("w1", PACK)
+        for t in range(PACK):
             nc.gpsimd.tensor_scalar(
-                w1_23[0][:, t * P : (t + 1) * P, :].rearrange("p (q r) j -> p q r j", r=8),
-                w1_raw[:].rearrange("p j (q t r) -> p t q r j", t=PACK, r=8)[:, 2 + t],
+                w1_all[0][:, t * P : (t + 1) * P, :].rearrange("p (q r) j -> p q r j", r=8),
+                w1_raw[:].rearrange("p j (q t r) -> p t q r j", t=PACK, r=8)[:, t],
                 1.0, 0.0, MULT, ADD,
             )
-        quantize_tiles(w1_23)
-        project(w1_23, 0, centre_banks[2], 0, T)
-        project(w1_23, 1, centre_banks[3], 0, T)
-        for t in range(1, PACK):
+        quantize_tiles(w1_all)
+        centre = [keep.tile([P, T], F32, name="centre%d" % t) for t in range(PACK)]
+        centre_banks = (banks[2], banks[4], banks[5], banks[6])
+        for t in range(PACK):
+            project(w1_all, t, centre_banks[t], 0, T)
             nc.scalar.copy(centre[t][:], centre_banks[t][:])
+            turn(centre[t], t, False, False)
+
+        excess = keep.tile([P, PACK, T], F32, name="excess")
+        for t in range(PACK):
+            nc.vector.tensor_tensor(w1_raw[:, t, :], windows[t][:].indirect(offsets[1][:]), first_list[t][:], SUB)
+            nc.scalar.activation(excess[:, t, :], w1_raw[:, t, :], RELU)
+            turn(excess[:, t, :], t, False, True)
+
+        w3_bf = keep.tile([P, N, PACK], BF16, name="w3_bf", tag="w1_plane", align_bytes=64)
+        w3_codes = keep.tile([P, N], U32, name="w3_codes", align_bytes=64)
+        w3_plane = keep.tile([P, N], U8, name="w3_plane", align_bytes=64)
+        nc.scalar.copy(w3_bf[:], w3_raw[:].rearrange("p j n -> p n j"))
+        quantize(w3_bf[:], w3_codes[:], w3_plane[:])
 
         halves = (slice(0, HALF), slice(HALF, T))
 
-        def gather(d):
-            edges = keep.tile([P, PACK, T], F32, name="edges%d" % d, tag="edges%d" % d, align_bytes=64)
-            steps = [(t, slice(0, T)) for t in range(PACK)]
-            if d == 1:
-                steps[0:1] = [(0, cols) for cols in halves]
+        def gather(d, edges, steps):
             for t, cols in steps:
                 picked = windows[t][:].indirect(offsets[d][:, cols.start // LIST_ROWS : cols.stop // LIST_ROWS])
                 nc.vector.tensor_tensor(edges[:, t, cols], picked, centre[t][:, cols], ADD)
-            return edges
 
         def round_relu(edges, dst, cols):
             nc.scalar.activation(
@@ -180,26 +179,17 @@ def tile_picked_wedgecv_relu_l_kernel(
                 RELU,
             )
 
-        rounded = [keep.tile([P, T, PACK], BF16, name="rounded%d" % d) for d in range(3)]
-        edges1 = gather(1)
+        edges2 = keep.tile([P, PACK, T], F32, name="edges2", tag="edges2", align_bytes=64)
+        whole = slice(0, T)
+        gather(2, edges2, [(t, whole) for t in range(PACK)])
+        gather(3, w1_raw, [(0, whole), (1, whole)] + [(t, cols) for cols in halves for t in (2, 3)])
 
-        back_banks = (banks[7], banks[1])
+        best01 = keep.tile([P, T, PACK], BF16, name="best01")
+        back_banks = (banks[2], banks[4])
         for u in range(2):
             for h in range(2):
-                bank = (banks[2], banks[4], banks[5], banks[6])[2 * u + h]
-                for b in range(2):
-                    cols = slice((2 * h + b) * P, (2 * h + b + 1) * P)
-                    for e in range(2):
-                        dst = bank[:, (2 * b + e) * P : (2 * b + e + 1) * P]
-                        t = 2 * u + e
-                        nc.tensor.matmul(
-                            dst, first_list[t][:, cols], identity[:], start=True, stop=False, is_transpose=True
-                        )
-                        nc.tensor.matmul(
-                            dst, centre[t][:, cols], identity[:], start=False, stop=True, is_transpose=True
-                        )
-                pairs = keep.tile([P, 2, P, 2], BF16, name="pairs%d%d" % (u, h))
-                nc.scalar.copy(pairs[:], bank[:].rearrange("v (b e p) -> v b p e", b=2, e=2))
+                pairs = keep.tile([P, 2, P, 2], BF16, name="pairs%d%d" % (u, h), tag="pairs%d%d" % (u, h))
+                nc.scalar.copy(pairs[:], sum_banks[2 * u + h][:].rearrange("v (b e p) -> v b p e", b=2, e=2))
                 words = pairs[:].rearrange("v b p e -> v (b p e)").bitcast(F32)
                 for b in range(2):
                     nc.tensor.transpose(
@@ -209,32 +199,21 @@ def tile_picked_wedgecv_relu_l_kernel(
                     )
         for h in range(2):
             nc.scalar.copy(
-                rounded[0][:, h * HALF : (h + 1) * HALF, :].bitcast(F32),
+                best01[:, h * HALF : (h + 1) * HALF, :].bitcast(F32),
                 back_banks[h][:].rearrange("p (u v) -> p v u", u=2),
             )
-        round_relu(edges1, rounded[1], slice(0, T))
-
-        w3_bf = keep.tile([P, N, PACK], BF16, name="w3_bf", tag="w1_23_codes", align_bytes=64)
-        w3_codes = keep.tile([P, N], U32, name="w3_codes", align_bytes=64)
-        w3_plane = keep.tile([P, N], U8, name="w3_plane", align_bytes=64)
-        nc.scalar.copy(w3_bf[:], w3_raw[:].rearrange("p j n -> p n j"))
-        quantize(w3_bf[:], w3_codes[:], w3_plane[:])
-
-        edges2 = gather(2)
-        round_relu(edges2, rounded[2], slice(0, T))
-        edges3 = gather(3)
-        last = keep.tile([P, T, PACK], BF16, name="rounded3")
+        rounded2 = keep.tile([P, T, PACK], BF16, name="rounded2", tag="pairs11")
+        round_relu(edges2, rounded2, slice(0, T))
+        last = keep.tile([P, T, PACK], BF16, name="rounded3", tag="edges2", align_bytes=64)
         for cols in halves:
-            round_relu(edges3, last, cols)
-        best01 = keep.tile([P, T, PACK], BF16, name="best01")
+            round_relu(w1_raw, last, cols)
         best012 = keep.tile([P, T, PACK], BF16, name="best012")
         z = keep.tile([P, T, PACK], BF16, name="z", align_bytes=64)
-        for dst, a, b in ((best01, rounded[0], rounded[1]), (best012, best01, rounded[2])):
-            for cols in halves:
-                nc.vector.tensor_tensor(dst[:, cols, :], a[:, cols, :], b[:, cols, :], MAX)
+        for cols in halves:
+            nc.vector.tensor_tensor(best012[:, cols, :], best01[:, cols, :], rounded2[:, cols, :], MAX)
 
         pieces = (slice(0, HALF), slice(HALF, HALF + P), slice(HALF + P, T))
-        out_banks = (banks[3], banks[0], banks[2])
+        out_banks = (banks[5], banks[6], banks[3])
         copies = (nc.scalar.copy, nc.vector.tensor_copy, nc.scalar.copy)
         stores = (nc.scalar.dma_start, nc.sync.dma_start, nc.scalar.dma_start)
 
@@ -245,8 +224,7 @@ def tile_picked_wedgecv_relu_l_kernel(
         def project_out(i):
             cols = pieces[i]
             count = cols.stop - cols.start
-            tag = "edges3" if i == 0 else "z_codes%d" % i
-            codes = keep.tile([P, count], U32, name="z_codes%d" % i, tag=tag, align_bytes=64)
+            codes = keep.tile([P, count], U32, name="z_codes%d" % i, align_bytes=64)
             plane = keep.tile([P, count], U8, name="z_plane%d" % i, align_bytes=64)
             result = keep.tile([P, count], F32, name="result%d" % i)
             quantize(z[:, cols, :], codes[:], plane[:])

@@ -49,7 +49,7 @@ def tile_picked_wedgecv_relu_l_kernel(
         nc.sync.dma_start(x_codes[:].bitcast(I32), x_words[0].bitcast(I32))
         offsets = [lists.tile([P, T // LIST_ROWS], U16, name="offsets%d" % d) for d in range(4)]
         nc.sync.dma_start(offsets[0][:], pos1)
-        w1_raw = keep.tile([P, PACK, H], F32, name="w1_raw")
+        w1_raw = keep.tile([P, PACK, H], F32, name="w1_raw", tag="w1_raw", align_bytes=64)
         nc.sync.dma_start(w1_raw[:], w1.rearrange("(p j) c -> p j c", j=PACK))
         for tile, pos in zip(offsets[1:], (pos2, pos3, pos4)):
             nc.sync.dma_start(tile[:], pos)
@@ -184,7 +184,6 @@ def tile_picked_wedgecv_relu_l_kernel(
         gather(2, edges2, [(t, whole) for t in range(PACK)])
         gather(3, w1_raw, [(0, whole), (1, whole)] + [(t, cols) for cols in halves for t in (2, 3)])
 
-        best01 = keep.tile([P, T, PACK], BF16, name="best01")
         back_banks = (banks[2], banks[4])
         for u in range(2):
             for h in range(2):
@@ -193,24 +192,20 @@ def tile_picked_wedgecv_relu_l_kernel(
                 words = pairs[:].rearrange("v b p e -> v (b p e)").bitcast(F32)
                 for b in range(2):
                     nc.tensor.transpose(
-                        back_banks[h][:, (2 * u + b) * P : (2 * u + b + 1) * P],
+                        back_banks[h][:].rearrange("p (v u) -> p u v", u=2)[:, u, b * P : (b + 1) * P],
                         words[:, b * P : (b + 1) * P],
                         identity[:],
                     )
-        for h in range(2):
-            nc.scalar.copy(
-                best01[:, h * HALF : (h + 1) * HALF, :].bitcast(F32),
-                back_banks[h][:].rearrange("p (u v) -> p v u", u=2),
-            )
-        rounded2 = keep.tile([P, T, PACK], BF16, name="rounded2", tag="pairs11")
+        rounded2 = keep.tile([P, T, PACK], BF16, name="rounded2", tag="pairs10")
         round_relu(edges2, rounded2, slice(0, T))
         last = keep.tile([P, T, PACK], BF16, name="rounded3", tag="edges2", align_bytes=64)
         for cols in halves:
             round_relu(w1_raw, last, cols)
         best012 = keep.tile([P, T, PACK], BF16, name="best012")
         z = keep.tile([P, T, PACK], BF16, name="z", align_bytes=64)
-        for cols in halves:
-            nc.vector.tensor_tensor(best012[:, cols, :], best01[:, cols, :], rounded2[:, cols, :], MAX)
+        for bank, cols in zip(back_banks, halves):
+            best01 = bank[:].bitcast(BF16).rearrange("p (v t) -> p v t", t=PACK)
+            nc.vector.tensor_tensor(best012[:, cols, :], best01, rounded2[:, cols, :], MAX)
 
         pieces = (slice(0, HALF), slice(HALF, HALF + P), slice(HALF + P, T))
         out_banks = (banks[5], banks[6], banks[3])
@@ -224,7 +219,8 @@ def tile_picked_wedgecv_relu_l_kernel(
         def project_out(i):
             cols = pieces[i]
             count = cols.stop - cols.start
-            codes = keep.tile([P, count], U32, name="z_codes%d" % i, align_bytes=64)
+            tag = "w1_raw" if i == 0 else "z_codes%d" % i
+            codes = keep.tile([P, count], U32, name="z_codes%d" % i, tag=tag, align_bytes=64)
             plane = keep.tile([P, count], U8, name="z_plane%d" % i, align_bytes=64)
             result = keep.tile([P, count], F32, name="result%d" % i)
             quantize(z[:, cols, :], codes[:], plane[:])

@@ -40,8 +40,9 @@ def tile_picked_wedgecv_relu_l_kernel(
         x_plane = keep.tile([P, T], U8, name="x_plane", align_bytes=64)
         nc.vector.memset(x_plane[:].bitcast(I32), 0)
 
-        w2_raw = keep.tile([P, PACK, H], F32, name="w2_raw")
-        nc.sync.dma_start(w2_raw[:], w2.rearrange("(p j) c -> p j c", j=PACK))
+        w2_rows = w2.rearrange("(p j) c -> p j c", j=PACK)
+        w2_raw = [keep.tile([P, PACK, H // 2], F32, name="w2_raw%d" % h) for h in range(2)]
+        nc.sync.dma_start(w2_raw[0][:], w2_rows[:, :, : H // 2])
         for q in range(4):
             nc.sync.dma_start(
                 x_plane[32 * q : 32 * q + 4, :].bitcast(I32), x_scales[0, 4 * q : 4 * q + 4, :].bitcast(I32)
@@ -49,6 +50,7 @@ def tile_picked_wedgecv_relu_l_kernel(
         nc.sync.dma_start(x_codes[:].bitcast(I32), x_words[0].bitcast(I32))
         offsets = [lists.tile([P, T // LIST_ROWS], U16, name="offsets%d" % d) for d in range(4)]
         nc.sync.dma_start(offsets[0][:], pos1)
+        nc.sync.dma_start(w2_raw[1][:], w2_rows[:, :, H // 2 :])
         w1_raw = keep.tile([P, PACK, H], F32, name="w1_raw", tag="w1_raw", align_bytes=64)
         nc.sync.dma_start(w1_raw[:], w1.rearrange("(p j) c -> p j c", j=PACK))
         for tile, pos in zip(offsets[1:], (pos2, pos3, pos4)):
@@ -63,14 +65,11 @@ def tile_picked_wedgecv_relu_l_kernel(
         for t in range(1, PACK):
             nc.vector.memset(windows[t][:, T:], 0.0)
         nc.scalar.activation(windows[0][:, T:], windows[1][:, T:], RELU)
+        dealt_windows = [keep.tile([P, T + LIST_ROWS], F32, name="dealt_window%d" % t) for t in range(PACK)]
+        for t in range(PACK):
+            nc.vector.memset(dealt_windows[t][:, T:], 0.0)
         identity = keep.tile([P, P], F32, name="identity")
         make_identity(nc, identity[:])
-
-        def deal(copy, raw, dealt, lo, hi, blocks=slice(0, 16)):
-            copy(
-                dealt.rearrange("p (t q r) j -> p q t r j", t=hi - lo, r=8)[:, blocks],
-                raw[:].rearrange("p j (q t r) -> p q t r j", t=PACK, r=8)[:, blocks, lo:hi],
-            )
 
         def quantize(dealt, codes, plane):
             nc.vector.quantize_mx(codes.bitcast(FP8X4), plane, dealt.rearrange("p m j -> p (m j)"))
@@ -87,8 +86,8 @@ def tile_picked_wedgecv_relu_l_kernel(
 
         banks = [psum.tile([P, T], F32, name="bank%d" % b) for b in range(8)]
 
-        def project(tiles, layer, bank, first, count):
-            cols = slice(layer * P, (layer + 1) * P)
+        def project(tiles, first_col, bank, first, count):
+            cols = slice(first_col, first_col + P)
             nc.tensor.matmul_mx(
                 bank[:, :count],
                 tiles[1][:, cols].bitcast(FP8X4),
@@ -99,65 +98,92 @@ def tile_picked_wedgecv_relu_l_kernel(
                 stop=True,
             )
 
-        w2_0, w2_1, w2_23 = mx_tiles("w2_0", 1), mx_tiles("w2_1", 1), mx_tiles("w2_23", 2)
-        deal(nc.vector.tensor_copy, w2_raw, w2_0[0], 0, 1, slice(0, 10))
-        deal(nc.scalar.copy, w2_raw, w2_0[0], 0, 1, slice(10, 16))
-        quantize_tiles(w2_0)
-        deal(nc.scalar.copy, w2_raw, w2_1[0], 1, 2)
-        deal(nc.vector.tensor_copy, w2_raw, w2_23[0], 2, 4)
-        quantize_tiles(w2_1)
-        quantize_tiles(w2_23)
+        w2_mx = [mx_tiles("w2_%d" % u, 2) for u in range(2)]
+
+        def deal(copy, u, h, blocks=slice(0, 8)):
+            raw = w2_raw[h][:].rearrange("p j (q u e r) -> p u e q r j", u=2, e=2, r=8)[:, u]
+            dealt = w2_mx[u][0][:, h * P : (h + 1) * P, :].rearrange("p (e q r) j -> p e q r j", e=2, r=8)
+            if h == 1:
+                raw = raw[:, ::-1]
+            copy(dealt[:, :, blocks], raw[:, :, blocks])
+
+        def quantize_half(u, h):
+            cols = slice(h * P, (h + 1) * P)
+            quantize(w2_mx[u][0][:, cols, :], w2_mx[u][1][:, cols], w2_mx[u][2][:, cols])
+
+        deal(nc.vector.tensor_copy, 0, 0, slice(0, 5))
+        deal(nc.scalar.copy, 0, 0, slice(5, 8))
+        quantize_half(0, 0)
+        deal(nc.scalar.copy, 1, 0)
+        quantize_half(1, 0)
         for bank, first, count in ((banks[0], 0, P), (banks[1], P, P), (banks[2], HALF, HALF)):
-            project(w2_0, 0, bank, first, count)
+            project(w2_mx[0], 0, bank, first, count)
             nc.scalar.copy(windows[0][:, first : first + count], bank[:, :count])
-        project(w2_1, 0, banks[4], 0, T)
-        project(w2_23, 0, banks[5], 0, T)
-        project(w2_23, 1, banks[6], 0, T)
+        project(w2_mx[1], 0, banks[4], 0, T)
+        for u in range(2):
+            deal(nc.vector.tensor_copy, u, 1)
+        for u in range(2):
+            quantize_half(u, 1)
+            project(w2_mx[u], P, banks[5 + u], 0, T)
 
-        first_list = [keep.tile([P, T], F32, name="first_list%d" % t) for t in range(PACK)]
-        for t in range(PACK):
-            if t > 0:
-                nc.scalar.copy(windows[t][:, :T], banks[3 + t][:])
-            nc.vector.tensor_copy(first_list[t][:], windows[t][:].indirect(offsets[0][:]))
-
-        sum_banks = (banks[3], banks[7], banks[0], banks[1])
-
-        def turn(src, t, start, stop):
-            u, e = divmod(t, 2)
-            for h in range(2):
-                for b in range(2):
-                    nc.tensor.matmul(
-                        sum_banks[2 * u + h][:, (2 * b + e) * P : (2 * b + e + 1) * P],
-                        src[:, (2 * h + b) * P : (2 * h + b + 1) * P],
-                        identity[:],
-                        start=start and e == 0 and b == 0,
-                        stop=stop and e == 1 and b == 1,
-                        is_transpose=True,
-                    )
-
-        for t in range(PACK):
-            turn(first_list[t], t, True, False)
+        reused = w2_raw[1][:].rearrange("p (a j) c -> p a (j c)", a=2)
+        first_list = [reused[:, 0], reused[:, 1]]
+        first_list += [keep.tile([P, T], F32, name="first_list%d" % a)[:] for a in (2, 3)]
+        for a in range(PACK):
+            if a > 0:
+                nc.scalar.copy(windows[a][:, :T], banks[3 + a][:])
+            nc.vector.tensor_copy(first_list[a], windows[a][:].indirect(offsets[0][:]))
 
         w1_all = mx_tiles("w1", PACK)
         for t in range(PACK):
-            nc.gpsimd.tensor_scalar(
-                w1_all[0][:, t * P : (t + 1) * P, :].rearrange("p (q r) j -> p q r j", r=8),
-                w1_raw[:].rearrange("p j (q t r) -> p t q r j", t=PACK, r=8)[:, t],
-                1.0, 0.0, MULT, ADD,
-            )
+            dealt = w1_all[0][:, t * P : (t + 1) * P, :].rearrange("p (q r) j -> p q r j", r=8)
+            raw = w1_raw[:].rearrange("p j (q t r) -> p t q r j", t=PACK, r=8)[:, t]
+            if t < PACK - 1:
+                nc.gpsimd.tensor_scalar(dealt, raw, 1.0, 0.0, MULT, ADD)
+            else:
+                nc.scalar.copy(dealt, raw)
+
+        for u, bank in ((0, banks[2]), (1, banks[4])):
+            project(w2_mx[u], P // 2, bank, 0, T)
+            nc.scalar.copy(dealt_windows[2 * u][: P // 2, :T], windows[u][: P // 2, :T])
+            nc.scalar.copy(dealt_windows[2 * u][P // 2 :, :T], windows[2 + u][P // 2 :, :T])
+            nc.scalar.copy(dealt_windows[2 * u + 1][:, :T], bank[:])
+
+        sum_banks = (banks[3], banks[7], banks[0], banks[1])
+
+        def turn(src, u, place, start, stop):
+            for h in range(2):
+                for b in range(2):
+                    block = sum_banks[2 * u + h][:].rearrange("v (b e g i) -> v b e g i", b=2, e=2, g=2)[:, b]
+                    nc.tensor.matmul(
+                        place(block),
+                        src[:, (2 * h + b) * P : (2 * h + b + 1) * P],
+                        identity[:],
+                        start=start and b == 0,
+                        stop=stop and b == 1,
+                        is_transpose=True,
+                    )
+
+        def turn_early(src, a, start, stop):
+            g, u = divmod(a, 2)
+            turn(src, u, (lambda v: v[:, :, 0], lambda v: v[:, ::-1, 1])[g], start and g == 0, stop and g == 1)
+
+        for a in range(PACK):
+            turn_early(first_list[a], a, True, False)
+
         quantize_tiles(w1_all)
         centre = [keep.tile([P, T], F32, name="centre%d" % t) for t in range(PACK)]
-        centre_banks = (banks[2], banks[4], banks[5], banks[6])
+        centre_banks = (banks[5], banks[6], banks[2], banks[4])
         for t in range(PACK):
-            project(w1_all, t, centre_banks[t], 0, T)
+            project(w1_all, t * P, centre_banks[t], 0, T)
             nc.scalar.copy(centre[t][:], centre_banks[t][:])
-            turn(centre[t], t, False, False)
+            turn(centre[t], t // 2, lambda v: v[:, t % 2], False, False)
 
         excess = keep.tile([P, PACK, T], F32, name="excess")
         for t in range(PACK):
-            nc.vector.tensor_tensor(w1_raw[:, t, :], windows[t][:].indirect(offsets[1][:]), first_list[t][:], SUB)
+            nc.vector.tensor_tensor(w1_raw[:, t, :], windows[t][:].indirect(offsets[1][:]), first_list[t], SUB)
             nc.scalar.activation(excess[:, t, :], w1_raw[:, t, :], RELU)
-            turn(excess[:, t, :], t, False, True)
+            turn_early(excess[:, t, :], t, False, True)
 
         w3_bf = keep.tile([P, N, PACK], BF16, name="w3_bf", tag="w1_plane", align_bytes=64)
         w3_codes = keep.tile([P, N], U32, name="w3_codes", align_bytes=64)
@@ -169,7 +195,7 @@ def tile_picked_wedgecv_relu_l_kernel(
 
         def gather(d, edges, steps):
             for t, cols in steps:
-                picked = windows[t][:].indirect(offsets[d][:, cols.start // LIST_ROWS : cols.stop // LIST_ROWS])
+                picked = dealt_windows[t][:].indirect(offsets[d][:, cols.start // LIST_ROWS : cols.stop // LIST_ROWS])
                 nc.vector.tensor_tensor(edges[:, t, cols], picked, centre[t][:, cols], ADD)
 
         def round_relu(edges, dst, cols):
@@ -184,7 +210,7 @@ def tile_picked_wedgecv_relu_l_kernel(
         gather(2, edges2, [(t, whole) for t in range(PACK)])
         gather(3, w1_raw, [(0, whole), (1, whole)] + [(t, cols) for cols in halves for t in (2, 3)])
 
-        back_banks = (banks[2], banks[4])
+        back_banks = (banks[5], banks[6])
         for u in range(2):
             for h in range(2):
                 pairs = keep.tile([P, 2, P, 2], BF16, name="pairs%d%d" % (u, h), tag="pairs%d%d" % (u, h))
@@ -208,7 +234,7 @@ def tile_picked_wedgecv_relu_l_kernel(
             nc.vector.tensor_tensor(best012[:, cols, :], best01, rounded2[:, cols, :], MAX)
 
         pieces = (slice(0, HALF), slice(HALF, HALF + P), slice(HALF + P, T))
-        out_banks = (banks[5], banks[6], banks[3])
+        out_banks = (banks[2], banks[4], banks[3])
         copies = (nc.scalar.copy, nc.vector.tensor_copy, nc.scalar.copy)
         stores = (nc.scalar.dma_start, nc.sync.dma_start, nc.scalar.dma_start)
 

@@ -1,7 +1,6 @@
 from contextlib import ExitStack
 
 import concourse.mybir as mybir
-from concourse.masks import make_identity
 
 K, T, H, N = 512, 512, 512, 128
 FLOPS = 2 * K * H * T * 2 + 2 * H * N * T
@@ -14,16 +13,16 @@ U16 = mybir.dt.uint16
 U8 = mybir.dt.uint8
 FP8X4 = mybir.dt.float8_e4m3fn_x4
 FP4X4 = mybir.dt.float4_e2m1fn_x4
-RELU = mybir.ActivationFunctionType.Relu
+COPY = mybir.ActivationFunctionType.Copy
 MULT = mybir.AluOpType.mult
 ADD = mybir.AluOpType.add
 MAX = mybir.AluOpType.max
-SUB = mybir.AluOpType.subtract
 
 P = 128
 PACK = 4
-WINDOW = 1024
 LIST_ROWS = 16
+VECTOR_WINDOW = 704
+SCALAR_WINDOW = T + LIST_ROWS
 HALF = T // 2
 
 
@@ -40,226 +39,153 @@ def tile_picked_wedgecv_relu_l_kernel(
         x_plane = keep.tile([P, T], U8, name="x_plane", align_bytes=64)
         nc.vector.memset(x_plane[:].bitcast(I32), 0)
 
-        w2_rows = w2.rearrange("(p j) c -> p j c", j=PACK)
-        w2_raw = [keep.tile([P, PACK, H // 2], F32, name="w2_raw%d" % h) for h in range(2)]
-        nc.sync.dma_start(w2_raw[0][:], w2_rows[:, :, : H // 2])
+        w2_raw = keep.tile([P, PACK, H], F32, name="w2_raw")
+        nc.sync.dma_start(w2_raw[:], w2.rearrange("(p j) c -> p j c", j=PACK))
         for q in range(4):
             nc.sync.dma_start(
                 x_plane[32 * q : 32 * q + 4, :].bitcast(I32), x_scales[0, 4 * q : 4 * q + 4, :].bitcast(I32)
             )
         nc.sync.dma_start(x_codes[:].bitcast(I32), x_words[0].bitcast(I32))
         offsets = [lists.tile([P, T // LIST_ROWS], U16, name="offsets%d" % d) for d in range(4)]
-        nc.sync.dma_start(offsets[0][:], pos1)
-        nc.sync.dma_start(w2_raw[1][:], w2_rows[:, :, H // 2 :])
-        w1_raw = keep.tile([P, PACK, H], F32, name="w1_raw", tag="w1_raw", align_bytes=64)
-        nc.sync.dma_start(w1_raw[:], w1.rearrange("(p j) c -> p j c", j=PACK))
-        for tile, pos in zip(offsets[1:], (pos2, pos3, pos4)):
+        for tile, pos in zip(offsets, (pos1, pos2, pos3, pos4)):
             nc.sync.dma_start(tile[:], pos)
+        w1_raw = keep.tile([P, PACK, H], F32, name="w1_raw")
+        nc.sync.dma_start(w1_raw[:], w1.rearrange("(p j) c -> p j c", j=PACK))
         w3_raw = keep.tile([P, PACK, N], F32, name="w3_raw")
-        for q in range(H // 32):
-            nc.sync.dma_start(
-                w3_raw[8 * q : 8 * q + 8], w3[32 * q : 32 * q + 32].rearrange("(t r) n -> r t n", t=PACK)
-            )
-
-        windows = [keep.tile([P, WINDOW], F32, name="window%d" % t) for t in range(PACK)]
-        for t in range(1, PACK):
-            nc.vector.memset(windows[t][:, T:], 0.0)
-        nc.scalar.activation(windows[0][:, T:], windows[1][:, T:], RELU)
-        dealt_windows = [keep.tile([P, T + LIST_ROWS], F32, name="dealt_window%d" % t) for t in range(PACK)]
+        w3_rows = w3.rearrange("(q t r) n -> t q r n", t=PACK, r=8)
         for t in range(PACK):
-            nc.vector.memset(dealt_windows[t][:, T:], 0.0)
-        identity = keep.tile([P, P], F32, name="identity")
-        make_identity(nc, identity[:])
+            nc.sync.dma_start(w3_raw[:, t, :], w3_rows[t])
 
-        def quantize(dealt, codes, plane):
-            nc.vector.quantize_mx(codes.bitcast(FP8X4), plane, dealt.rearrange("p m j -> p (m j)"))
+        windows = [
+            keep.tile([P, SCALAR_WINDOW if t else VECTOR_WINDOW], F32, name="window%d" % t) for t in range(PACK)
+        ]
+        nc.vector.memset(windows[0][:, T:], 0.0)
+        for t in range(1, PACK):
+            nc.scalar.activation(windows[t][:, T:], windows[0][:, T:SCALAR_WINDOW], COPY)
 
-        def mx_tiles(name, layers):
+        def mx_tiles(name, columns):
             return (
-                keep.tile([P, layers * P, PACK], BF16, name=name + "_bf", align_bytes=64)[:],
-                keep.tile([P, layers * P], U32, name=name + "_codes", align_bytes=64),
-                keep.tile([P, layers * P], U8, name=name + "_plane", tag=name + "_plane", align_bytes=64),
+                keep.tile([P, columns, PACK], BF16, name=name + "_bf", align_bytes=64),
+                keep.tile([P, columns], U32, name=name + "_codes", align_bytes=64),
+                keep.tile([P, columns], U8, name=name + "_plane", align_bytes=64),
             )
 
-        def quantize_tiles(tiles):
-            quantize(tiles[0], tiles[1][:], tiles[2][:])
+        def quantize(tiles):
+            nc.vector.quantize_mx(tiles[1][:].bitcast(FP8X4), tiles[2][:], tiles[0][:].rearrange("p m j -> p (m j)"))
+
+        def layer_views(raw, rounded, t):
+            return (
+                rounded.rearrange("p (q r) j -> p q r j", r=8),
+                raw[:].rearrange("p j (q t r) -> p t q r j", t=PACK, r=8)[:, t],
+            )
 
         banks = [psum.tile([P, T], F32, name="bank%d" % b) for b in range(8)]
 
-        def project(tiles, first_col, bank, first, count):
+        def project(tiles, first_col, bank):
             cols = slice(first_col, first_col + P)
             nc.tensor.matmul_mx(
-                bank[:, :count],
+                bank[:],
                 tiles[1][:, cols].bitcast(FP8X4),
                 tiles[2][:, cols],
-                x_codes[:, 2 * first : 2 * (first + count)].bitcast(FP4X4),
-                x_plane[:, first : first + count],
+                x_codes[:].bitcast(FP4X4),
+                x_plane[:],
                 start=True,
                 stop=True,
             )
 
-        w2_mx = [mx_tiles("w2_%d" % u, 2) for u in range(2)]
-
-        def deal(copy, u, h, blocks=slice(0, 8)):
-            raw = w2_raw[h][:].rearrange("p j (q u e r) -> p u e q r j", u=2, e=2, r=8)[:, u]
-            dealt = w2_mx[u][0][:, h * P : (h + 1) * P, :].rearrange("p (e q r) j -> p e q r j", e=2, r=8)
-            if h == 1:
-                raw = raw[:, ::-1]
-            copy(dealt[:, :, blocks], raw[:, :, blocks])
-
-        def quantize_half(u, h):
-            cols = slice(h * P, (h + 1) * P)
-            quantize(w2_mx[u][0][:, cols, :], w2_mx[u][1][:, cols], w2_mx[u][2][:, cols])
-
-        deal(nc.vector.tensor_copy, 0, 0, slice(0, 5))
-        deal(nc.scalar.copy, 0, 0, slice(5, 8))
-        quantize_half(0, 0)
-        deal(nc.scalar.copy, 1, 0)
-        quantize_half(1, 0)
-        for bank, first, count in ((banks[0], 0, P), (banks[1], P, P), (banks[2], HALF, HALF)):
-            project(w2_mx[0], 0, bank, first, count)
-            nc.scalar.copy(windows[0][:, first : first + count], bank[:, :count])
-        project(w2_mx[1], 0, banks[4], 0, T)
-        for u in range(2):
-            deal(nc.vector.tensor_copy, u, 1)
-        for u in range(2):
-            quantize_half(u, 1)
-            project(w2_mx[u], P, banks[5 + u], 0, T)
-
-        reused = w2_raw[1][:].rearrange("p (a j) c -> p a (j c)", a=2)
-        first_list = [reused[:, 0], reused[:, 1]]
-        first_list += [keep.tile([P, T], F32, name="first_list%d" % a)[:] for a in (2, 3)]
-        for a in range(PACK):
-            if a > 0:
-                nc.scalar.copy(windows[a][:, :T], banks[3 + a][:])
-            nc.vector.tensor_copy(first_list[a], windows[a][:].indirect(offsets[0][:]))
-
-        w1_all = mx_tiles("w1", PACK)
+        w2_mx = [mx_tiles("w2_%d" % t, P) for t in range(PACK)]
+        views = [layer_views(w2_raw, w2_mx[t][0][:], t) for t in range(PACK)]
+        nc.vector.tensor_copy(views[0][0][:, :10], views[0][1][:, :10])
+        nc.scalar.copy(views[0][0][:, 10:], views[0][1][:, 10:])
+        nc.scalar.copy(*views[1])
+        quantize(w2_mx[0])
+        nc.vector.tensor_copy(*views[2])
+        quantize(w2_mx[1])
+        nc.vector.tensor_copy(*views[3])
+        quantize(w2_mx[2])
+        quantize(w2_mx[3])
         for t in range(PACK):
-            dealt = w1_all[0][:, t * P : (t + 1) * P, :].rearrange("p (q r) j -> p q r j", r=8)
-            raw = w1_raw[:].rearrange("p j (q t r) -> p t q r j", t=PACK, r=8)[:, t]
-            if t < PACK - 1:
-                nc.gpsimd.tensor_scalar(dealt, raw, 1.0, 0.0, MULT, ADD)
-            else:
-                nc.scalar.copy(dealt, raw)
+            project(w2_mx[t], 0, banks[t])
+            nc.scalar.copy(windows[t][:, :T], banks[t][:])
 
-        for u, bank in ((0, banks[2]), (1, banks[4])):
-            project(w2_mx[u], P // 2, bank, 0, T)
-            nc.scalar.copy(dealt_windows[2 * u][: P // 2, :T], windows[u][: P // 2, :T])
-            nc.scalar.copy(dealt_windows[2 * u][P // 2 :, :T], windows[2 + u][P // 2 :, :T])
-            nc.scalar.copy(dealt_windows[2 * u + 1][:, :T], bank[:])
-
-        sum_banks = (banks[3], banks[7], banks[0], banks[1])
-
-        def turn(src, u, place, start, stop):
-            for h in range(2):
-                for b in range(2):
-                    block = sum_banks[2 * u + h][:].rearrange("v (b e g i) -> v b e g i", b=2, e=2, g=2)[:, b]
-                    nc.tensor.matmul(
-                        place(block),
-                        src[:, (2 * h + b) * P : (2 * h + b + 1) * P],
-                        identity[:],
-                        start=start and b == 0,
-                        stop=stop and b == 1,
-                        is_transpose=True,
-                    )
-
-        def turn_early(src, a, start, stop):
-            g, u = divmod(a, 2)
-            turn(src, u, (lambda v: v[:, :, 0], lambda v: v[:, ::-1, 1])[g], start and g == 0, stop and g == 1)
-
-        for a in range(PACK):
-            turn_early(first_list[a], a, True, False)
-
-        quantize_tiles(w1_all)
-        centre = [keep.tile([P, T], F32, name="centre%d" % t) for t in range(PACK)]
-        centre_banks = (banks[5], banks[6], banks[2], banks[4])
-        for t in range(PACK):
-            project(w1_all, t * P, centre_banks[t], 0, T)
-            nc.scalar.copy(centre[t][:], centre_banks[t][:])
-            turn(centre[t], t // 2, lambda v: v[:, t % 2], False, False)
-
-        excess = keep.tile([P, PACK, T], F32, name="excess")
-        for t in range(PACK):
-            nc.vector.tensor_tensor(w1_raw[:, t, :], windows[t][:].indirect(offsets[1][:]), first_list[t], SUB)
-            nc.scalar.activation(excess[:, t, :], w1_raw[:, t, :], RELU)
-            turn_early(excess[:, t, :], t, False, True)
-
-        w3_bf = keep.tile([P, N, PACK], BF16, name="w3_bf", tag="w1_plane", align_bytes=64)
-        w3_codes = keep.tile([P, N], U32, name="w3_codes", align_bytes=64)
-        w3_plane = keep.tile([P, N], U8, name="w3_plane", align_bytes=64)
-        nc.scalar.copy(w3_bf[:], w3_raw[:].rearrange("p j n -> p n j"))
-        quantize(w3_bf[:], w3_codes[:], w3_plane[:])
-
-        halves = (slice(0, HALF), slice(HALF, T))
-
-        def gather(d, edges, steps):
-            for t, cols in steps:
-                picked = dealt_windows[t][:].indirect(offsets[d][:, cols.start // LIST_ROWS : cols.stop // LIST_ROWS])
-                nc.vector.tensor_tensor(edges[:, t, cols], picked, centre[t][:, cols], ADD)
-
-        def round_relu(edges, dst, cols):
-            nc.scalar.activation(
-                dst[:, cols, :].rearrange("p (c i) t -> p c t i", i=4),
-                edges[:, :, cols].rearrange("p t (c i) -> p c t i", i=4),
-                RELU,
-            )
-
-        edges2 = keep.tile([P, PACK, T], F32, name="edges2", tag="edges2", align_bytes=64)
+        picked = [keep.tile([P, 4, T], F32, name="picked%d" % t) for t in range(PACK)]
         whole = slice(0, T)
-        gather(2, edges2, [(t, whole) for t in range(PACK)])
-        gather(3, w1_raw, [(0, whole), (1, whole)] + [(t, cols) for cols in halves for t in (2, 3)])
-
-        back_banks = (banks[5], banks[6])
-        for u in range(2):
-            for h in range(2):
-                pairs = keep.tile([P, 2, P, 2], BF16, name="pairs%d%d" % (u, h), tag="pairs%d%d" % (u, h))
-                nc.scalar.copy(pairs[:], sum_banks[2 * u + h][:].rearrange("v (b e p) -> v b p e", b=2, e=2))
-                words = pairs[:].rearrange("v b p e -> v (b p e)").bitcast(F32)
-                for b in range(2):
-                    nc.tensor.transpose(
-                        back_banks[h][:].rearrange("p (v u) -> p u v", u=2)[:, u, b * P : (b + 1) * P],
-                        words[:, b * P : (b + 1) * P],
-                        identity[:],
-                    )
-        rounded2 = keep.tile([P, T, PACK], BF16, name="rounded2", tag="pairs10")
-        round_relu(edges2, rounded2, slice(0, T))
-        last = keep.tile([P, T, PACK], BF16, name="rounded3", tag="edges2", align_bytes=64)
-        for cols in halves:
-            round_relu(w1_raw, last, cols)
-        best012 = keep.tile([P, T, PACK], BF16, name="best012")
-        z = keep.tile([P, T, PACK], BF16, name="z", align_bytes=64)
-        for bank, cols in zip(back_banks, halves):
-            best01 = bank[:].bitcast(BF16).rearrange("p (v t) -> p v t", t=PACK)
-            nc.vector.tensor_tensor(best012[:, cols, :], best01, rounded2[:, cols, :], MAX)
-
         pieces = (slice(0, HALF), slice(HALF, HALF + P), slice(HALF + P, T))
-        out_banks = (banks[2], banks[4], banks[3])
-        copies = (nc.scalar.copy, nc.vector.tensor_copy, nc.scalar.copy)
-        stores = (nc.scalar.dma_start, nc.sync.dma_start, nc.scalar.dma_start)
 
-        def best_of_all(i):
-            cols = pieces[i]
-            nc.vector.tensor_tensor(z[:, cols, :], best012[:, cols, :], last[:, cols, :], MAX)
+        def looked_up(t, d, cols):
+            return windows[t][:].indirect(offsets[d][:, cols.start // LIST_ROWS : cols.stop // LIST_ROWS])
+
+        for d in range(4):
+            nc.vector.tensor_copy(picked[0][:, d, :], looked_up(0, d, whole))
+        for t, cols in [(1, whole), (2, whole)] + [(3, piece) for piece in pieces]:
+            for d in range(4):
+                nc.scalar.activation(picked[t][:, d, cols], looked_up(t, d, cols), COPY)
+
+        w1_mx = mx_tiles("w1", H)
+        for t in range(PACK):
+            nc.gpsimd.tensor_scalar(*layer_views(w1_raw, w1_mx[0][:, t * P : (t + 1) * P, :], t), 1.0, 0.0, MULT, ADD)
+        w3_mx = mx_tiles("w3", N)
+        nc.gpsimd.tensor_scalar(w3_mx[0][:], w3_raw[:].rearrange("p j n -> p n j"), 1.0, 0.0, MULT, ADD)
+        quantize(w1_mx)
+        for t in range(PACK):
+            project(w1_mx, t * P, banks[4 + t])
+
+        edge = keep.tile([P, PACK, T], BF16, name="edge")
+
+        def larger_of_pairs(t, cols):
+            nc.vector.tensor_tensor(picked[t][:, :2, cols], picked[t][:, :2, cols], picked[t][:, 2:, cols], MAX)
+
+        def largest(t, cols):
+            nc.vector.tensor_tensor(picked[t][:, 0, cols], picked[t][:, 0, cols], picked[t][:, 1, cols], MAX)
+
+        def add_centre(t, cols):
+            nc.vector.tensor_tensor(edge[:, t, cols], banks[4 + t][:, cols], picked[t][:, 0, cols], ADD)
+
+        z_mx = [mx_tiles("z%d" % i, cols.stop - cols.start) for i, cols in enumerate(pieces)]
+
+        def relu_weave(i):
+            nc.vector.tensor_scalar(
+                z_mx[i][0][:].rearrange("p (c i) t -> p c t i", i=4),
+                edge[:, :, pieces[i]].rearrange("p t (c i) -> p c t i", i=4),
+                0.0,
+                None,
+                MAX,
+            )
 
         def project_out(i):
             cols = pieces[i]
             count = cols.stop - cols.start
-            tag = "w1_raw" if i == 0 else "z_codes%d" % i
-            codes = keep.tile([P, count], U32, name="z_codes%d" % i, tag=tag, align_bytes=64)
-            plane = keep.tile([P, count], U8, name="z_plane%d" % i, align_bytes=64)
             result = keep.tile([P, count], F32, name="result%d" % i)
-            quantize(z[:, cols, :], codes[:], plane[:])
+            quantize(z_mx[i])
             nc.tensor.matmul_mx(
-                out_banks[i][:, :count], w3_codes[:].bitcast(FP8X4), w3_plane[:], codes[:].bitcast(FP8X4), plane[:],
+                banks[i][:, :count], w3_mx[1][:].bitcast(FP8X4), w3_mx[2][:], z_mx[i][1][:].bitcast(FP8X4), z_mx[i][2][:],
                 start=True, stop=True,
             )
-            copies[i](result[:], out_banks[i][:, :count])
-            stores[i](out[:, cols], result[:])
+            nc.scalar.copy(result[:], banks[i][:, :count])
+            nc.sync.dma_start(out[:, cols], result[:])
 
-        best_of_all(0)
-        best_of_all(1)
+        larger_of_pairs(0, whole)
+        larger_of_pairs(1, whole)
+        largest(0, whole)
+        largest(1, whole)
+        add_centre(0, whole)
+        larger_of_pairs(2, whole)
+        add_centre(1, whole)
+        largest(2, whole)
+        quantize(w3_mx)
+        larger_of_pairs(3, pieces[0])
+        add_centre(2, whole)
+        largest(3, pieces[0])
+        larger_of_pairs(3, pieces[1])
+        add_centre(3, pieces[0])
+        largest(3, pieces[1])
+        relu_weave(0)
+        add_centre(3, pieces[1])
         project_out(0)
-        best_of_all(2)
+        larger_of_pairs(3, pieces[2])
+        relu_weave(1)
+        largest(3, pieces[2])
         project_out(1)
+        add_centre(3, pieces[2])
+        relu_weave(2)
         project_out(2)

@@ -24,6 +24,7 @@ LIST_ROWS = 16
 VECTOR_WINDOW = 704
 SCALAR_WINDOW = T + LIST_ROWS
 HALF = T // 2
+SHARE = 320
 
 
 def tile_picked_wedgecv_relu_l_kernel(
@@ -39,19 +40,22 @@ def tile_picked_wedgecv_relu_l_kernel(
         x_plane = keep.tile([P, T], U8, name="x_plane", align_bytes=64)
         nc.vector.memset(x_plane[:].bitcast(I32), 0)
 
-        w2_raw = keep.tile([P, PACK, H], F32, name="w2_raw")
-        nc.sync.dma_start(w2_raw[:], w2.rearrange("(p j) c -> p j c", j=PACK))
+        w2_rows = w2.rearrange("(p j) c -> p j c", j=PACK)
+        w2_raw = [keep.tile([P, PACK, H // 2], F32, name="w2_raw%d" % h) for h in range(2)]
+        for h in range(2):
+            nc.sync.dma_start(w2_raw[h][:], w2_rows[:, :, h * H // 2 : (h + 1) * H // 2])
         for q in range(4):
             nc.sync.dma_start(
                 x_plane[32 * q : 32 * q + 4, :].bitcast(I32), x_scales[0, 4 * q : 4 * q + 4, :].bitcast(I32)
             )
         nc.sync.dma_start(x_codes[:].bitcast(I32), x_words[0].bitcast(I32))
         offsets = [lists.tile([P, T // LIST_ROWS], U16, name="offsets%d" % d) for d in range(4)]
-        for tile, pos in zip(offsets, (pos1, pos2, pos3, pos4)):
-            nc.sync.dma_start(tile[:], pos)
-        w1_raw = keep.tile([P, PACK, H], F32, name="w1_raw")
+        nc.sync.dma_start(offsets[0][:], pos1)
+        w1_raw = keep.tile([P, PACK, H], F32, name="w1_raw", tag="w1_raw")
         nc.sync.dma_start(w1_raw[:], w1.rearrange("(p j) c -> p j c", j=PACK))
-        w3_raw = keep.tile([P, PACK, N], F32, name="w3_raw")
+        for tile, pos in zip(offsets[1:], (pos2, pos3, pos4)):
+            nc.sync.dma_start(tile[:], pos)
+        w3_raw = keep.tile([P, PACK, N], F32, name="w3_raw", tag="w3_raw")
         w3_rows = w3.rearrange("(q t r) n -> t q r n", t=PACK, r=8)
         for t in range(PACK):
             nc.sync.dma_start(w3_raw[:, t, :], w3_rows[t])
@@ -65,8 +69,8 @@ def tile_picked_wedgecv_relu_l_kernel(
 
         def mx_tiles(name, columns):
             return (
-                keep.tile([P, columns, PACK], BF16, name=name + "_bf", align_bytes=64),
-                keep.tile([P, columns], U32, name=name + "_codes", align_bytes=64),
+                keep.tile([P, columns, PACK], BF16, name=name + "_bf", tag=name + "_bf", align_bytes=64),
+                keep.tile([P, columns], U32, name=name + "_codes", tag=name + "_codes", align_bytes=64),
                 keep.tile([P, columns], U8, name=name + "_plane", align_bytes=64),
             )
 
@@ -81,72 +85,85 @@ def tile_picked_wedgecv_relu_l_kernel(
 
         banks = [psum.tile([P, T], F32, name="bank%d" % b) for b in range(8)]
 
-        def project(tiles, first_col, bank):
-            cols = slice(first_col, first_col + P)
+        def project(tiles, first_col, dst, cols):
+            layer = slice(first_col, first_col + P)
             nc.tensor.matmul_mx(
-                bank[:],
-                tiles[1][:, cols].bitcast(FP8X4),
-                tiles[2][:, cols],
-                x_codes[:].bitcast(FP4X4),
-                x_plane[:],
+                dst,
+                tiles[1][:, layer].bitcast(FP8X4),
+                tiles[2][:, layer],
+                x_codes[:, 2 * cols.start : 2 * cols.stop].bitcast(FP4X4),
+                x_plane[:, cols],
                 start=True,
                 stop=True,
             )
 
-        w2_mx = [mx_tiles("w2_%d" % t, P) for t in range(PACK)]
-        views = [layer_views(w2_raw, w2_mx[t][0][:], t) for t in range(PACK)]
-        nc.vector.tensor_copy(views[0][0][:, :10], views[0][1][:, :10])
-        nc.scalar.copy(views[0][0][:, 10:], views[0][1][:, 10:])
-        nc.scalar.copy(*views[1])
-        quantize(w2_mx[0])
-        nc.vector.tensor_copy(*views[2])
-        quantize(w2_mx[1])
-        nc.vector.tensor_copy(*views[3])
-        quantize(w2_mx[2])
-        quantize(w2_mx[3])
-        for t in range(PACK):
-            project(w2_mx[t], 0, banks[t])
-            nc.scalar.copy(windows[t][:, :T], banks[t][:])
-
-        picked = [keep.tile([P, 4, T], F32, name="picked%d" % t) for t in range(PACK)]
         whole = slice(0, T)
-        pieces = (slice(0, HALF), slice(HALF, HALF + P), slice(HALF + P, T))
+        halves = (slice(0, HALF), slice(HALF, T))
+        w2_first = mx_tiles("w2_first", P)
+        w2_rest = mx_tiles("w2_rest", 3 * P)
 
-        def looked_up(t, d, cols):
-            return windows[t][:].indirect(offsets[d][:, cols.start // LIST_ROWS : cols.stop // LIST_ROWS])
+        def deal(copy, h, first, last):
+            tiles, base = (w2_first, 0) if first == 0 else (w2_rest, 1)
+            dealt = tiles[0][:].rearrange("p (t h q r) j -> p h q t r j", h=2, q=8, r=8)[:, h, :, first - base : last - base]
+            raw = w2_raw[h][:].rearrange("p j (q t r) -> p q t r j", t=PACK, r=8)[:, :, first:last]
+            copy(dealt, raw)
 
-        for d in range(4):
-            nc.vector.tensor_copy(picked[0][:, d, :], looked_up(0, d, whole))
-        for t, cols in [(1, whole), (2, whole)] + [(3, piece) for piece in pieces]:
-            for d in range(4):
-                nc.scalar.activation(picked[t][:, d, cols], looked_up(t, d, cols), COPY)
+        deal(nc.vector.tensor_copy, 0, 0, 1)
+        deal(nc.vector.tensor_copy, 0, 1, 4)
+        deal(nc.vector.tensor_copy, 1, 0, 1)
+        deal(nc.scalar.copy, 1, 1, 3)
+        deal(nc.vector.tensor_copy, 1, 3, 4)
+        quantize(w2_first)
+        quantize(w2_rest)
+        for bank, cols, copy in zip((banks[0], banks[7]), halves, (nc.scalar.copy, nc.vector.tensor_copy)):
+            project(w2_first, 0, bank[:, :HALF], cols)
+            copy(windows[0][:, cols], bank[:, :HALF])
+        for t in (1, 3, 2):
+            project(w2_rest, (t - 1) * P, banks[t][:], whole)
+            nc.scalar.copy(windows[t][:, :T], banks[t][:])
 
         w1_mx = mx_tiles("w1", H)
         for t in range(PACK):
             nc.gpsimd.tensor_scalar(*layer_views(w1_raw, w1_mx[0][:, t * P : (t + 1) * P, :], t), 1.0, 0.0, MULT, ADD)
         w3_mx = mx_tiles("w3", N)
         nc.gpsimd.tensor_scalar(w3_mx[0][:], w3_raw[:].rearrange("p j n -> p n j"), 1.0, 0.0, MULT, ADD)
+
+        tags = ("picked0", "picked1", "w3_raw", "w1_raw")
+        picked = [keep.tile([P, 4, T], F32, name="picked%d" % t, tag=tags[t]) for t in range(PACK)]
+        pieces = (slice(0, HALF), slice(HALF, HALF + P), slice(HALF + P, T))
+
+        def looked_up(t, d, cols):
+            return windows[t][:].indirect(offsets[d][:, cols.start // LIST_ROWS : cols.stop // LIST_ROWS])
+
+        by_vector, by_scalar = slice(0, SHARE), slice(SHARE, T)
+        for t, d, cols in [(0, 0, whole), (1, 0, by_vector)] + [(0, d, whole) for d in range(1, 4)]:
+            nc.vector.tensor_copy(picked[t][:, d, cols], looked_up(t, d, cols))
+        steps = [(1, 0, by_scalar)] + [(1, d, whole) for d in range(1, 4)] + [(3, d, whole) for d in range(4)]
+        for t, d, cols in steps + [(2, d, piece) for piece in pieces for d in range(4)]:
+            nc.scalar.activation(picked[t][:, d, cols], looked_up(t, d, cols), COPY)
+
         quantize(w1_mx)
-        for t in range(PACK):
-            project(w1_mx, t * P, banks[4 + t])
+        for u in range(2):
+            for h in range(2):
+                for e in range(2):
+                    project(w1_mx, (2 * u + e) * P, banks[4 + 2 * u + h][:, e * HALF : (e + 1) * HALF], halves[h])
 
-        edge = keep.tile([P, PACK, T], BF16, name="edge")
+        edges = keep.tile([P, 2, T, 2], BF16, name="edges")
 
-        def larger_of_pairs(t, cols):
-            nc.vector.tensor_tensor(picked[t][:, :2, cols], picked[t][:, :2, cols], picked[t][:, 2:, cols], MAX)
+        def larger(dst, a, b):
+            nc.vector.tensor_tensor(dst, a, b, MAX)
 
-        def largest(t, cols):
-            nc.vector.tensor_tensor(picked[t][:, 0, cols], picked[t][:, 0, cols], picked[t][:, 1, cols], MAX)
-
-        def add_centre(t, cols):
-            nc.vector.tensor_tensor(edge[:, t, cols], banks[4 + t][:, cols], picked[t][:, 0, cols], ADD)
+        def add_centre(u, best, cols):
+            h, first = divmod(cols.start, HALF)
+            centre = banks[4 + 2 * u + h][:].rearrange("p (e v) -> p v e", e=2)[:, first : first + cols.stop - cols.start]
+            nc.vector.tensor_tensor(edges[:, u, cols], centre, best[:, :, cols].rearrange("p e v -> p v e"), ADD)
 
         z_mx = [mx_tiles("z%d" % i, cols.stop - cols.start) for i, cols in enumerate(pieces)]
 
         def relu_weave(i):
             nc.vector.tensor_scalar(
-                z_mx[i][0][:].rearrange("p (c i) t -> p c t i", i=4),
-                edge[:, :, pieces[i]].rearrange("p t (c i) -> p c t i", i=4),
+                z_mx[i][0][:].rearrange("p v (u e) -> p v u e", u=2),
+                edges[:, :, pieces[i]].rearrange("p u v e -> p v u e"),
                 0.0,
                 None,
                 MAX,
@@ -164,28 +181,39 @@ def tile_picked_wedgecv_relu_l_kernel(
             nc.scalar.copy(result[:], banks[i][:, :count])
             nc.sync.dma_start(out[:, cols], result[:])
 
-        larger_of_pairs(0, whole)
-        larger_of_pairs(1, whole)
-        largest(0, whole)
-        largest(1, whole)
-        add_centre(0, whole)
-        larger_of_pairs(2, whole)
-        add_centre(1, whole)
-        largest(2, whole)
+        pairs = keep.tile([P, 2, 2, T], F32, name="pairs", tag="w1_bf", align_bytes=64)
+        best01 = picked[0][:, :2]
+        best23 = picked[0][:, 1::2]
+
+        def chain(i, d):
+            best = best23[:, 0, pieces[i]]
+            larger(best, best if d > 1 else picked[2][:, 0, pieces[i]], picked[2][:, d, pieces[i]])
+
+        for t in range(2):
+            larger(pairs[:, t], picked[t][:, :2], picked[t][:, 2:])
+        larger(best01[:, 0], pairs[:, 0, 0], pairs[:, 0, 1])
+        larger(best23[:, 1], picked[3][:, 0], picked[3][:, 1])
+        larger(best01[:, 1], pairs[:, 1, 0], pairs[:, 1, 1])
+        larger(best23[:, 1], best23[:, 1], picked[3][:, 2])
+        add_centre(0, best01, halves[0])
+        larger(best23[:, 1], best23[:, 1], picked[3][:, 3])
+        chain(0, 1)
+        add_centre(0, best01, halves[1])
+        chain(0, 2)
         quantize(w3_mx)
-        larger_of_pairs(3, pieces[0])
-        add_centre(2, whole)
-        largest(3, pieces[0])
-        larger_of_pairs(3, pieces[1])
-        add_centre(3, pieces[0])
-        largest(3, pieces[1])
+        chain(0, 3)
+        chain(1, 1)
+        add_centre(1, best23, pieces[0])
+        chain(1, 2)
         relu_weave(0)
-        add_centre(3, pieces[1])
+        chain(1, 3)
         project_out(0)
-        larger_of_pairs(3, pieces[2])
+        add_centre(1, best23, pieces[1])
+        chain(2, 1)
         relu_weave(1)
-        largest(3, pieces[2])
+        chain(2, 2)
         project_out(1)
-        add_centre(3, pieces[2])
+        chain(2, 3)
+        add_centre(1, best23, pieces[2])
         relu_weave(2)
         project_out(2)

@@ -24,7 +24,7 @@ LIST_ROWS = 16
 VECTOR_WINDOW = 704
 SCALAR_WINDOW = T + LIST_ROWS
 HALF = T // 2
-SHARE = 320
+SHARE = 96
 
 
 def tile_picked_wedgecv_relu_l_kernel(
@@ -61,10 +61,11 @@ def tile_picked_wedgecv_relu_l_kernel(
             nc.sync.dma_start(w3_raw[:, t, :], w3_rows[t])
 
         windows = [
-            keep.tile([P, SCALAR_WINDOW if t else VECTOR_WINDOW], F32, name="window%d" % t) for t in range(PACK)
+            keep.tile([P, SCALAR_WINDOW if t > 1 else VECTOR_WINDOW], F32, name="window%d" % t) for t in range(PACK)
         ]
-        nc.vector.memset(windows[0][:, T:], 0.0)
-        for t in range(1, PACK):
+        for t in range(2):
+            nc.vector.memset(windows[t][:, T:], 0.0)
+        for t in range(2, PACK):
             nc.scalar.activation(windows[t][:, T:], windows[0][:, T:SCALAR_WINDOW], COPY)
 
         def mx_tiles(name, columns):
@@ -74,8 +75,10 @@ def tile_picked_wedgecv_relu_l_kernel(
                 keep.tile([P, columns], U8, name=name + "_plane", align_bytes=64),
             )
 
-        def quantize(tiles):
-            nc.vector.quantize_mx(tiles[1][:].bitcast(FP8X4), tiles[2][:], tiles[0][:].rearrange("p m j -> p (m j)"))
+        def quantize(tiles, cols=slice(None)):
+            nc.vector.quantize_mx(
+                tiles[1][:, cols].bitcast(FP8X4), tiles[2][:, cols], tiles[0][:, cols].rearrange("p m j -> p (m j)")
+            )
 
         def layer_views(raw, rounded, t):
             return (
@@ -99,27 +102,26 @@ def tile_picked_wedgecv_relu_l_kernel(
 
         whole = slice(0, T)
         halves = (slice(0, HALF), slice(HALF, T))
-        w2_first = mx_tiles("w2_first", P)
-        w2_rest = mx_tiles("w2_rest", 3 * P)
+        groups = ((0, 1), (1, 2), (2, 4))
+        w2_mx = [mx_tiles("w2_%d" % first, (last - first) * P) for first, last in groups]
 
-        def deal(copy, h, first, last):
-            tiles, base = (w2_first, 0) if first == 0 else (w2_rest, 1)
-            dealt = tiles[0][:].rearrange("p (t h q r) j -> p h q t r j", h=2, q=8, r=8)[:, h, :, first - base : last - base]
+        def deal(copy, h, g):
+            first, last = groups[g]
+            dealt = w2_mx[g][0][:].rearrange("p (t h q r) j -> p h q t r j", h=2, q=8, r=8)[:, h]
             raw = w2_raw[h][:].rearrange("p j (q t r) -> p q t r j", t=PACK, r=8)[:, :, first:last]
             copy(dealt, raw)
 
-        deal(nc.vector.tensor_copy, 0, 0, 1)
-        deal(nc.vector.tensor_copy, 0, 1, 4)
-        deal(nc.vector.tensor_copy, 1, 0, 1)
-        deal(nc.scalar.copy, 1, 1, 3)
-        deal(nc.vector.tensor_copy, 1, 3, 4)
-        quantize(w2_first)
-        quantize(w2_rest)
+        for g in range(3):
+            deal(nc.vector.tensor_copy, 0, g)
+        for g, copy in enumerate((nc.vector.tensor_copy, nc.vector.tensor_copy, nc.scalar.copy)):
+            deal(copy, 1, g)
+        for tiles in w2_mx:
+            quantize(tiles)
         for bank, cols, copy in zip((banks[0], banks[7]), halves, (nc.scalar.copy, nc.vector.tensor_copy)):
-            project(w2_first, 0, bank[:, :HALF], cols)
+            project(w2_mx[0], 0, bank[:, :HALF], cols)
             copy(windows[0][:, cols], bank[:, :HALF])
-        for t in (1, 3, 2):
-            project(w2_rest, (t - 1) * P, banks[t][:], whole)
+        for t, tiles, first_col in ((1, w2_mx[1], 0), (3, w2_mx[2], P), (2, w2_mx[2], 0)):
+            project(tiles, first_col, banks[t][:], whole)
             nc.scalar.copy(windows[t][:, :T], banks[t][:])
 
         w1_mx = mx_tiles("w1", H)
@@ -128,19 +130,21 @@ def tile_picked_wedgecv_relu_l_kernel(
         w3_mx = mx_tiles("w3", N)
         nc.gpsimd.tensor_scalar(w3_mx[0][:], w3_raw[:].rearrange("p j n -> p n j"), 1.0, 0.0, MULT, ADD)
 
-        tags = ("picked0", "picked1", "w3_raw", "w1_raw")
+        tags = ("picked0", "picked1", "picked1", "w1_raw")
         picked = [keep.tile([P, 4, T], F32, name="picked%d" % t, tag=tags[t]) for t in range(PACK)]
-        pieces = (slice(0, HALF), slice(HALF, HALF + P), slice(HALF + P, T))
 
         def looked_up(t, d, cols):
             return windows[t][:].indirect(offsets[d][:, cols.start // LIST_ROWS : cols.stop // LIST_ROWS])
 
-        by_vector, by_scalar = slice(0, SHARE), slice(SHARE, T)
-        for t, d, cols in [(0, 0, whole), (1, 0, by_vector)] + [(0, d, whole) for d in range(1, 4)]:
-            nc.vector.tensor_copy(picked[t][:, d, cols], looked_up(t, d, cols))
-        steps = [(1, 0, by_scalar)] + [(1, d, whole) for d in range(1, 4)] + [(3, d, whole) for d in range(4)]
-        for t, d, cols in steps + [(2, d, piece) for piece in pieces for d in range(4)]:
+        def fetch(t, d, cols):
             nc.scalar.activation(picked[t][:, d, cols], looked_up(t, d, cols), COPY)
+
+        for t, d in [(0, 0), (1, 0), (0, 1), (0, 2), (0, 3)]:
+            nc.vector.tensor_copy(picked[t][:, d, :], looked_up(t, d, whole))
+        nc.vector.tensor_copy(picked[1][:, 1, :SHARE], looked_up(1, 1, slice(0, SHARE)))
+        fetch(1, 1, slice(SHARE, T))
+        for t, d in [(1, 2), (1, 3)] + [(3, d) for d in range(4)]:
+            fetch(t, d, whole)
 
         quantize(w1_mx)
         for u in range(2):
@@ -158,62 +162,66 @@ def tile_picked_wedgecv_relu_l_kernel(
             centre = banks[4 + 2 * u + h][:].rearrange("p (e v) -> p v e", e=2)[:, first : first + cols.stop - cols.start]
             nc.vector.tensor_tensor(edges[:, u, cols], centre, best[:, :, cols].rearrange("p e v -> p v e"), ADD)
 
-        z_mx = [mx_tiles("z%d" % i, cols.stop - cols.start) for i, cols in enumerate(pieces)]
+        z_mx = [mx_tiles("z%d" % i, cols.stop - cols.start) for i, cols in enumerate(halves)]
 
         def relu_weave(i):
             nc.vector.tensor_scalar(
                 z_mx[i][0][:].rearrange("p v (u e) -> p v u e", u=2),
-                edges[:, :, pieces[i]].rearrange("p u v e -> p v u e"),
+                edges[:, :, halves[i]].rearrange("p u v e -> p v u e"),
                 0.0,
                 None,
                 MAX,
             )
 
-        def project_out(i):
-            cols = pieces[i]
-            count = cols.stop - cols.start
-            result = keep.tile([P, count], F32, name="result%d" % i)
-            quantize(z_mx[i])
+        def project_out(h, part, bank, copy, store):
+            count = part.stop - part.start
+            result = keep.tile([P, count], F32, name="result%d_%d" % (h, part.start))
+            quantize(z_mx[h], part)
             nc.tensor.matmul_mx(
-                banks[i][:, :count], w3_mx[1][:].bitcast(FP8X4), w3_mx[2][:], z_mx[i][1][:].bitcast(FP8X4), z_mx[i][2][:],
-                start=True, stop=True,
+                bank[:, :count],
+                w3_mx[1][:].bitcast(FP8X4),
+                w3_mx[2][:],
+                z_mx[h][1][:, part].bitcast(FP8X4),
+                z_mx[h][2][:, part],
+                start=True,
+                stop=True,
             )
-            nc.scalar.copy(result[:], banks[i][:, :count])
-            nc.sync.dma_start(out[:, cols], result[:])
+            copy(result[:], bank[:, :count])
+            store(out[:, h * HALF + part.start : h * HALF + part.stop], result[:])
 
         pairs = keep.tile([P, 2, 2, T], F32, name="pairs", tag="w1_bf", align_bytes=64)
         best01 = picked[0][:, :2]
         best23 = picked[0][:, 1::2]
 
-        def chain(i, d):
-            best = best23[:, 0, pieces[i]]
-            larger(best, best if d > 1 else picked[2][:, 0, pieces[i]], picked[2][:, d, pieces[i]])
-
         for t in range(2):
             larger(pairs[:, t], picked[t][:, :2], picked[t][:, 2:])
-        larger(best01[:, 0], pairs[:, 0, 0], pairs[:, 0, 1])
-        larger(best23[:, 1], picked[3][:, 0], picked[3][:, 1])
-        larger(best01[:, 1], pairs[:, 1, 0], pairs[:, 1, 1])
-        larger(best23[:, 1], best23[:, 1], picked[3][:, 2])
+        for d in range(2):
+            fetch(2, d, whole)
+        for cols in halves:
+            for d in (2, 3):
+                fetch(2, d, cols)
+        for t in range(2):
+            larger(best01[:, t], pairs[:, t, 0], pairs[:, t, 1])
+        quantize(w3_mx)
+        larger(picked[3][:, :2], picked[3][:, :2], picked[3][:, 2:])
         add_centre(0, best01, halves[0])
-        larger(best23[:, 1], best23[:, 1], picked[3][:, 3])
+        larger(best23[:, 1], picked[3][:, 0], picked[3][:, 1])
+
+        def chain(h, d):
+            best = best23[:, 0, halves[h]]
+            larger(best, best if d > 1 else picked[2][:, 0, halves[h]], picked[2][:, d, halves[h]])
+
         chain(0, 1)
         add_centre(0, best01, halves[1])
         chain(0, 2)
-        quantize(w3_mx)
-        chain(0, 3)
         chain(1, 1)
-        add_centre(1, best23, pieces[0])
+        chain(0, 3)
         chain(1, 2)
-        relu_weave(0)
+        add_centre(1, best23, halves[0])
         chain(1, 3)
-        project_out(0)
-        add_centre(1, best23, pieces[1])
-        chain(2, 1)
+        relu_weave(0)
+        add_centre(1, best23, halves[1])
+        project_out(0, slice(0, HALF), banks[0], nc.scalar.copy, nc.sync.dma_start)
         relu_weave(1)
-        chain(2, 2)
-        project_out(1)
-        chain(2, 3)
-        add_centre(1, best23, pieces[2])
-        relu_weave(2)
-        project_out(2)
+        project_out(1, slice(0, P), banks[1], nc.vector.tensor_copy, nc.sync.dma_start)
+        project_out(1, slice(P, HALF), banks[2], nc.scalar.copy, nc.scalar.dma_start)

@@ -41,9 +41,9 @@ def tile_picked_wedgecv_relu_l_kernel(
         nc.vector.memset(x_plane[:].bitcast(I32), 0)
 
         w2_rows = w2.rearrange("(p j) c -> p j c", j=PACK)
-        w2_raw = [keep.tile([P, PACK, H // 2], F32, name="w2_raw%d" % h) for h in range(2)]
+        w2_raw = [keep.tile([P, 2, H], F32, name="w2_raw%d" % h) for h in range(2)]
         for h in range(2):
-            nc.sync.dma_start(w2_raw[h][:], w2_rows[:, :, h * H // 2 : (h + 1) * H // 2])
+            nc.sync.dma_start(w2_raw[h][:], w2_rows[:, 2 * h : 2 * h + 2])
         for q in range(4):
             nc.sync.dma_start(
                 x_plane[32 * q : 32 * q + 4, :].bitcast(I32), x_scales[0, 4 * q : 4 * q + 4, :].bitcast(I32)
@@ -107,7 +107,7 @@ def tile_picked_wedgecv_relu_l_kernel(
 
         def deal(copy, h, g):
             first, last = groups[g]
-            dealt = w2_mx[g][0][:].rearrange("p (t h q r) j -> p h q t r j", h=2, q=8, r=8)[:, h]
+            dealt = w2_mx[g][0][:, :, 2 * h : 2 * h + 2].rearrange("p (t q r) j -> p q t r j", q=16, r=8)
             raw = w2_raw[h][:].rearrange("p j (q t r) -> p q t r j", t=PACK, r=8)[:, :, first:last]
             copy(dealt, raw)
 
@@ -162,32 +162,30 @@ def tile_picked_wedgecv_relu_l_kernel(
             centre = banks[4 + 2 * u + h][:].rearrange("p (e v) -> p v e", e=2)[:, first : first + cols.stop - cols.start]
             nc.vector.tensor_tensor(edges[:, u, cols], centre, best[:, :, cols].rearrange("p e v -> p v e"), ADD)
 
-        z_mx = [mx_tiles("z%d" % i, cols.stop - cols.start) for i, cols in enumerate(halves)]
-
-        def relu_weave(i):
+        def relu_weave(tiles, cols):
             nc.vector.tensor_scalar(
-                z_mx[i][0][:].rearrange("p v (u e) -> p v u e", u=2),
-                edges[:, :, halves[i]].rearrange("p u v e -> p v u e"),
+                tiles[0][:].rearrange("p v (u e) -> p v u e", u=2),
+                edges[:, :, cols].rearrange("p u v e -> p v u e"),
                 0.0,
                 None,
                 MAX,
             )
 
-        def project_out(h, part, bank, copy, store):
-            count = part.stop - part.start
-            result = keep.tile([P, count], F32, name="result%d_%d" % (h, part.start))
-            quantize(z_mx[h], part)
+        def project_out(tiles, cols, bank, copy, store):
+            count = cols.stop - cols.start
+            result = keep.tile([P, count], F32, name="result%d" % cols.start)
+            quantize(tiles)
             nc.tensor.matmul_mx(
                 bank[:, :count],
                 w3_mx[1][:].bitcast(FP8X4),
                 w3_mx[2][:],
-                z_mx[h][1][:, part].bitcast(FP8X4),
-                z_mx[h][2][:, part],
+                tiles[1][:].bitcast(FP8X4),
+                tiles[2][:],
                 start=True,
                 stop=True,
             )
             copy(result[:], bank[:, :count])
-            store(out[:, h * HALF + part.start : h * HALF + part.stop], result[:])
+            store(out[:, cols], result[:])
 
         pairs = keep.tile([P, 2, 2, T], F32, name="pairs", tag="w1_bf", align_bytes=64)
         best01 = picked[0][:, :2]
@@ -197,9 +195,9 @@ def tile_picked_wedgecv_relu_l_kernel(
             larger(pairs[:, t], picked[t][:, :2], picked[t][:, 2:])
         for d in range(2):
             fetch(2, d, whole)
-        for cols in halves:
-            for d in (2, 3):
-                fetch(2, d, cols)
+        pieces = (halves[0], slice(HALF, HALF + P), slice(HALF + P, T))
+        for d, cols in ((2, halves[0]), (3, halves[0]), (2, halves[1]), (3, pieces[1]), (3, pieces[2])):
+            fetch(2, d, cols)
         for t in range(2):
             larger(best01[:, t], pairs[:, t, 0], pairs[:, t, 1])
         quantize(w3_mx)
@@ -207,21 +205,25 @@ def tile_picked_wedgecv_relu_l_kernel(
         add_centre(0, best01, halves[0])
         larger(best23[:, 1], picked[3][:, 0], picked[3][:, 1])
 
-        def chain(h, d):
-            best = best23[:, 0, halves[h]]
-            larger(best, best if d > 1 else picked[2][:, 0, halves[h]], picked[2][:, d, halves[h]])
+        def chain(cols, d):
+            best = best23[:, 0, cols]
+            larger(best, best if d > 1 else picked[2][:, 0, cols], picked[2][:, d, cols])
 
-        chain(0, 1)
+        z_mx = [mx_tiles("z%d" % i, cols.stop - cols.start) for i, cols in enumerate(pieces)]
+        chain(halves[0], 1)
         add_centre(0, best01, halves[1])
-        chain(0, 2)
-        chain(1, 1)
-        chain(0, 3)
-        chain(1, 2)
+        chain(halves[0], 2)
+        chain(halves[1], 1)
+        chain(halves[0], 3)
+        chain(halves[1], 2)
         add_centre(1, best23, halves[0])
-        chain(1, 3)
-        relu_weave(0)
-        add_centre(1, best23, halves[1])
-        project_out(0, slice(0, HALF), banks[0], nc.scalar.copy, nc.sync.dma_start)
-        relu_weave(1)
-        project_out(1, slice(0, P), banks[1], nc.vector.tensor_copy, nc.sync.dma_start)
-        project_out(1, slice(P, HALF), banks[2], nc.scalar.copy, nc.scalar.dma_start)
+        chain(pieces[1], 3)
+        relu_weave(z_mx[0], pieces[0])
+        chain(pieces[2], 3)
+        add_centre(1, best23, pieces[1])
+        project_out(z_mx[0], pieces[0], banks[0], nc.scalar.copy, nc.sync.dma_start)
+        add_centre(1, best23, pieces[2])
+        relu_weave(z_mx[1], pieces[1])
+        relu_weave(z_mx[2], pieces[2])
+        project_out(z_mx[1], pieces[1], banks[1], nc.vector.tensor_copy, nc.sync.dma_start)
+        project_out(z_mx[2], pieces[2], banks[2], nc.scalar.copy, nc.scalar.dma_start)

@@ -51,8 +51,9 @@ def tile_picked_wedgecv_relu_l_kernel(
         nc.sync.dma_start(x_codes[:].bitcast(I32), x_words[0].bitcast(I32))
         offsets = [lists.tile([P, T // LIST_ROWS], U16, name="offsets%d" % d) for d in range(4)]
         nc.sync.dma_start(offsets[0][:], pos1)
-        w1_raw = keep.tile([P, PACK, H], F32, name="w1_raw", tag="w1_raw")
-        nc.sync.dma_start(w1_raw[:], w1.rearrange("(p j) c -> p j c", j=PACK))
+        w1_rows = keep.tile([P, PACK + 1, H], F32, name="w1_rows")
+        w1_raw = w1_rows[:, 1:]
+        nc.sync.dma_start(w1_raw, w1.rearrange("(p j) c -> p j c", j=PACK))
         for tile, pos in zip(offsets[1:], (pos2, pos3, pos4)):
             nc.sync.dma_start(tile[:], pos)
         w3_raw = keep.tile([P, PACK, N], F32, name="w3_raw", tag="w3_raw")
@@ -83,7 +84,7 @@ def tile_picked_wedgecv_relu_l_kernel(
         def layer_views(raw, rounded, t):
             return (
                 rounded.rearrange("p (q r) j -> p q r j", r=8),
-                raw[:].rearrange("p j (q t r) -> p t q r j", t=PACK, r=8)[:, t],
+                raw.rearrange("p j (q t r) -> p t q r j", t=PACK, r=8)[:, t],
             )
 
         banks = [psum.tile([P, T], F32, name="bank%d" % b) for b in range(8)]
@@ -111,10 +112,9 @@ def tile_picked_wedgecv_relu_l_kernel(
             raw = w2_raw[h][:].rearrange("p j (q t r) -> p q t r j", t=PACK, r=8)[:, :, first:last]
             copy(dealt, raw)
 
-        for g in range(3):
-            deal(nc.vector.tensor_copy, 0, g)
-        for g, copy in enumerate((nc.vector.tensor_copy, nc.vector.tensor_copy, nc.scalar.copy)):
-            deal(copy, 1, g)
+        for h in range(2):
+            for g, copy in enumerate((nc.vector.tensor_copy, nc.vector.tensor_copy, nc.scalar.copy)):
+                deal(copy, h, g)
         for tiles in w2_mx:
             quantize(tiles)
         for bank, cols, copy in zip((banks[0], banks[7]), halves, (nc.scalar.copy, nc.vector.tensor_copy)):
@@ -130,8 +130,9 @@ def tile_picked_wedgecv_relu_l_kernel(
         w3_mx = mx_tiles("w3", N)
         nc.gpsimd.tensor_scalar(w3_mx[0][:], w3_raw[:].rearrange("p j n -> p n j"), 1.0, 0.0, MULT, ADD)
 
-        tags = ("picked0", "picked1", "picked1", "w1_raw")
-        picked = [keep.tile([P, 4, T], F32, name="picked%d" % t, tag=tags[t]) for t in range(PACK)]
+        tags = ("picked0", "picked1", "picked1")
+        picked = [keep.tile([P, 4, T], F32, name="picked%d" % t, tag=tags[t]) for t in range(3)]
+        picked.append(w1_rows[:, :4])
 
         def looked_up(t, d, cols):
             return windows[t][:].indirect(offsets[d][:, cols.start // LIST_ROWS : cols.stop // LIST_ROWS])
@@ -142,8 +143,9 @@ def tile_picked_wedgecv_relu_l_kernel(
         for t, d in [(0, 0), (1, 0), (0, 1), (0, 2), (0, 3)]:
             nc.vector.tensor_copy(picked[t][:, d, :], looked_up(t, d, whole))
         nc.vector.tensor_copy(picked[1][:, 1, :SHARE], looked_up(1, 1, slice(0, SHARE)))
+        fetch(3, 0, whole)
         fetch(1, 1, slice(SHARE, T))
-        for t, d in [(1, 2), (1, 3)] + [(3, d) for d in range(4)]:
+        for t, d in [(1, 2), (1, 3)] + [(3, d) for d in range(1, 4)]:
             fetch(t, d, whole)
 
         quantize(w1_mx)

@@ -24,7 +24,6 @@ LIST_ROWS = 16
 VECTOR_WINDOW = 704
 SCALAR_WINDOW = T + LIST_ROWS
 HALF = T // 2
-SHARE = 96
 
 
 def tile_picked_wedgecv_relu_l_kernel(
@@ -142,10 +141,7 @@ def tile_picked_wedgecv_relu_l_kernel(
 
         for t, d in [(0, 0), (1, 0), (0, 1), (0, 2), (0, 3)]:
             nc.vector.tensor_copy(picked[t][:, d, :], looked_up(t, d, whole))
-        nc.vector.tensor_copy(picked[1][:, 1, :SHARE], looked_up(1, 1, slice(0, SHARE)))
-        fetch(3, 0, whole)
-        fetch(1, 1, slice(SHARE, T))
-        for t, d in [(1, 2), (1, 3)] + [(3, d) for d in range(1, 4)]:
+        for t, d in [(3, 0)] + [(t, d) for t in (1, 3) for d in range(1, 4)]:
             fetch(t, d, whole)
 
         quantize(w1_mx)
@@ -195,36 +191,39 @@ def tile_picked_wedgecv_relu_l_kernel(
 
         for t in range(2):
             larger(pairs[:, t], picked[t][:, :2], picked[t][:, 2:])
-        for d in range(2):
-            fetch(2, d, whole)
         pieces = (halves[0], slice(HALF, HALF + P), slice(HALF + P, T))
-        for d, cols in ((2, halves[0]), (3, halves[0]), (2, halves[1]), (3, pieces[1]), (3, pieces[2])):
-            fetch(2, d, cols)
+        for d in range(4):
+            fetch(2, d, halves[0])
+        for d in range(3):
+            fetch(2, d, halves[1])
+        for cols in pieces[1:]:
+            fetch(2, 3, cols)
         for t in range(2):
             larger(best01[:, t], pairs[:, t, 0], pairs[:, t, 1])
-        quantize(w3_mx)
-        larger(picked[3][:, :2], picked[3][:, :2], picked[3][:, 2:])
-        add_centre(0, best01, halves[0])
-        larger(best23[:, 1], picked[3][:, 0], picked[3][:, 1])
 
-        def chain(cols, d):
-            best = best23[:, 0, cols]
-            larger(best, best if d > 1 else picked[2][:, 0, cols], picked[2][:, d, cols])
+        def chain(e, cols, d):
+            best = best23[:, e, cols]
+            larger(best, best if d > 1 else picked[2 + e][:, 0, cols], picked[2 + e][:, d, cols])
 
         z_mx = [mx_tiles("z%d" % i, cols.stop - cols.start) for i, cols in enumerate(pieces)]
-        chain(halves[0], 1)
+        chain(1, whole, 1)
+        add_centre(0, best01, halves[0])
+        chain(1, whole, 2)
+        chain(0, halves[0], 1)
+        chain(1, whole, 3)
+        chain(0, halves[0], 2)
+        quantize(w3_mx)
+        chain(0, halves[0], 3)
         add_centre(0, best01, halves[1])
-        chain(halves[0], 2)
-        chain(halves[1], 1)
-        chain(halves[0], 3)
-        chain(halves[1], 2)
         add_centre(1, best23, halves[0])
-        chain(pieces[1], 3)
+        chain(0, halves[1], 1)
         relu_weave(z_mx[0], pieces[0])
-        chain(pieces[2], 3)
-        add_centre(1, best23, pieces[1])
+        chain(0, halves[1], 2)
         project_out(z_mx[0], pieces[0], banks[0], nc.scalar.copy, nc.sync.dma_start)
-        add_centre(1, best23, pieces[2])
+        for cols in pieces[1:]:
+            chain(0, cols, 3)
+        for cols in pieces[1:]:
+            add_centre(1, best23, cols)
         relu_weave(z_mx[1], pieces[1])
         relu_weave(z_mx[2], pieces[2])
         project_out(z_mx[1], pieces[1], banks[1], nc.vector.tensor_copy, nc.sync.dma_start)

@@ -116,7 +116,7 @@ def tile_picked_wedgecv_relu_l_kernel(
                 deal(copy, h, g)
         for tiles in w2_mx:
             quantize(tiles)
-        for bank, cols, copy in zip((banks[0], banks[7]), halves, (nc.scalar.copy, nc.vector.tensor_copy)):
+        for bank, cols, copy in zip((banks[0], banks[7]), halves, (nc.vector.tensor_copy, nc.scalar.copy)):
             project(w2_mx[0], 0, bank[:, :HALF], cols)
             copy(windows[0][:, cols], bank[:, :HALF])
         for t, tiles, first_col in ((1, w2_mx[1], 0), (3, w2_mx[2], P), (2, w2_mx[2], 0)):
@@ -185,7 +185,7 @@ def tile_picked_wedgecv_relu_l_kernel(
             copy(result[:], bank[:, :count])
             store(out[:, cols], result[:])
 
-        pairs = keep.tile([P, 2, 2, T], F32, name="pairs", tag="w1_bf", align_bytes=64)
+        pairs = keep.tile([P, 2, 2, T], F32, name="pairs", tag="w3_raw")
         best01 = picked[0][:, :2]
         best23 = picked[0][:, 1::2]
 

@@ -105,21 +105,27 @@ def tile_picked_wedgecv_relu_l_kernel(
         groups = ((0, 1), (1, 2), (2, 4))
         w2_mx = [mx_tiles("w2_%d" % first, (last - first) * P) for first, last in groups]
 
-        def deal(copy, h, g):
+        def deal(copy, h, g, blocks=slice(0, 16)):
             first, last = groups[g]
             dealt = w2_mx[g][0][:, :, 2 * h : 2 * h + 2].rearrange("p (t q r) j -> p q t r j", q=16, r=8)
             raw = w2_raw[h][:].rearrange("p j (q t r) -> p q t r j", t=PACK, r=8)[:, :, first:last]
-            copy(dealt, raw)
+            copy(dealt[:, blocks], raw[:, blocks])
 
-        for h in range(2):
-            for g, copy in enumerate((nc.vector.tensor_copy, nc.vector.tensor_copy, nc.scalar.copy)):
-                deal(copy, h, g)
+        for g, copy in enumerate((nc.vector.tensor_copy, nc.vector.tensor_copy, nc.scalar.copy)):
+            deal(copy, 0, g)
+        deal(nc.vector.tensor_copy, 1, 0, slice(0, 8))
+        deal(nc.scalar.copy, 1, 0, slice(8, 16))
+        deal(nc.vector.tensor_copy, 1, 1)
+        deal(nc.scalar.copy, 1, 2)
         for tiles in w2_mx:
             quantize(tiles)
         for bank, cols, copy in zip((banks[0], banks[7]), halves, (nc.vector.tensor_copy, nc.scalar.copy)):
             project(w2_mx[0], 0, bank[:, :HALF], cols)
             copy(windows[0][:, cols], bank[:, :HALF])
-        for t, tiles, first_col in ((1, w2_mx[1], 0), (3, w2_mx[2], P), (2, w2_mx[2], 0)):
+        for bank, cols in zip((banks[1], banks[6]), halves):
+            project(w2_mx[1], 0, bank[:, :HALF], cols)
+            nc.scalar.copy(windows[1][:, cols], bank[:, :HALF])
+        for t, tiles, first_col in ((3, w2_mx[2], P), (2, w2_mx[2], 0)):
             project(tiles, first_col, banks[t][:], whole)
             nc.scalar.copy(windows[t][:, :T], banks[t][:])
 

@@ -50,8 +50,8 @@ def tile_picked_wedgecv_relu_l_kernel(
         nc.sync.dma_start(x_codes[:].bitcast(I32), x_words[0].bitcast(I32))
         offsets = [lists.tile([P, T // LIST_ROWS], U16, name="offsets%d" % d) for d in range(4)]
         nc.sync.dma_start(offsets[0][:], pos1)
-        w1_rows = keep.tile([P, PACK + 1, H], F32, name="w1_rows")
-        w1_raw = w1_rows[:, 1:]
+        w1_rows = keep.tile([P, PACK, H], F32, name="w1_rows", tag="w1_rows", align_bytes=64)
+        w1_raw = w1_rows[:]
         nc.sync.dma_start(w1_raw, w1.rearrange("(p j) c -> p j c", j=PACK))
         for tile, pos in zip(offsets[1:], (pos2, pos3, pos4)):
             nc.sync.dma_start(tile[:], pos)
@@ -68,10 +68,10 @@ def tile_picked_wedgecv_relu_l_kernel(
         for t in range(2, PACK):
             nc.scalar.activation(windows[t][:, T:], windows[0][:, T:SCALAR_WINDOW], COPY)
 
-        def mx_tiles(name, columns):
+        def mx_tiles(name, columns, slot=None):
             return (
                 keep.tile([P, columns, PACK], BF16, name=name + "_bf", tag=name + "_bf", align_bytes=64),
-                keep.tile([P, columns], U32, name=name + "_codes", tag=name + "_codes", align_bytes=64),
+                keep.tile([P, columns], U32, name=name + "_codes", tag=slot or name + "_codes", align_bytes=64),
                 keep.tile([P, columns], U8, name=name + "_plane", align_bytes=64),
             )
 
@@ -132,12 +132,11 @@ def tile_picked_wedgecv_relu_l_kernel(
         w1_mx = mx_tiles("w1", H)
         for t in range(PACK):
             nc.gpsimd.tensor_scalar(*layer_views(w1_raw, w1_mx[0][:, t * P : (t + 1) * P, :], t), 1.0, 0.0, MULT, ADD)
-        w3_mx = mx_tiles("w3", N)
+        w3_mx = mx_tiles("w3", N, "w1_rows")
         nc.gpsimd.tensor_scalar(w3_mx[0][:], w3_raw[:].rearrange("p j n -> p n j"), 1.0, 0.0, MULT, ADD)
 
-        tags = ("picked0", "picked1", "picked1")
-        picked = [keep.tile([P, 4, T], F32, name="picked%d" % t, tag=tags[t]) for t in range(3)]
-        picked.append(w1_rows[:, :4])
+        early = keep.tile([P, 2, 4, T], F32, name="early")
+        picked = [early[:, 0], early[:, 1], early[:, 1], w1_raw]
 
         def looked_up(t, d, cols):
             return windows[t][:].indirect(offsets[d][:, cols.start // LIST_ROWS : cols.stop // LIST_ROWS])
@@ -147,7 +146,7 @@ def tile_picked_wedgecv_relu_l_kernel(
 
         for t, d in [(0, 0), (1, 0), (0, 1), (0, 2), (0, 3)]:
             nc.vector.tensor_copy(picked[t][:, d, :], looked_up(t, d, whole))
-        for t, d in [(3, 0)] + [(t, d) for t in (1, 3) for d in range(1, 4)]:
+        for t, d in [(1, d) for d in range(1, 4)] + [(3, d) for d in range(4)]:
             fetch(t, d, whole)
 
         quantize(w1_mx)
@@ -164,7 +163,7 @@ def tile_picked_wedgecv_relu_l_kernel(
         def add_centre(u, best, cols):
             h, first = divmod(cols.start, HALF)
             centre = banks[4 + 2 * u + h][:].rearrange("p (e v) -> p v e", e=2)[:, first : first + cols.stop - cols.start]
-            nc.vector.tensor_tensor(edges[:, u, cols], centre, best[:, :, cols].rearrange("p e v -> p v e"), ADD)
+            nc.vector.tensor_tensor(edges[:, u, cols], centre, best.rearrange("p e v -> p v e"), ADD)
 
         def relu_weave(tiles, cols):
             nc.vector.tensor_scalar(
@@ -191,12 +190,14 @@ def tile_picked_wedgecv_relu_l_kernel(
             copy(result[:], bank[:, :count])
             store(out[:, cols], result[:])
 
-        pairs = keep.tile([P, 2, 2, T], F32, name="pairs", tag="w3_raw")
+        maxima = keep.tile([P, 5, T], F32, name="maxima", tag="w3_raw")
+        pairs = maxima[:, :4].rearrange("p (t k) v -> p t k v", k=2)
+        partial3 = maxima[:, 4]
+        rows = early[:].rearrange("p t d (h v) -> p (t d h) v", h=2)
         best01 = picked[0][:, :2]
-        best23 = picked[0][:, 1::2]
+        best23 = (rows[:, 4:7:2], rows[:, 14:6:-7])
 
-        for t in range(2):
-            larger(pairs[:, t], picked[t][:, :2], picked[t][:, 2:])
+        larger(pairs, early[:, :, :2], early[:, :, 2:])
         pieces = (halves[0], slice(HALF, HALF + P), slice(HALF + P, T))
         for d in range(4):
             fetch(2, d, halves[0])
@@ -204,32 +205,35 @@ def tile_picked_wedgecv_relu_l_kernel(
             fetch(2, d, halves[1])
         for cols in pieces[1:]:
             fetch(2, 3, cols)
-        for t in range(2):
-            larger(best01[:, t], pairs[:, t, 0], pairs[:, t, 1])
 
-        def chain(e, cols, d):
-            best = best23[:, e, cols]
-            larger(best, best if d > 1 else picked[2 + e][:, 0, cols], picked[2 + e][:, d, cols])
+        def late_best(cols):
+            h, first = divmod(cols.start, HALF)
+            return best23[h][:, :, first : first + cols.stop - cols.start]
+
+        def chain(cols, d):
+            best = late_best(cols)[:, 0]
+            larger(best, best if d > 1 else picked[2][:, 0, cols], picked[2][:, d, cols])
 
         z_mx = [mx_tiles("z%d" % i, cols.stop - cols.start) for i, cols in enumerate(pieces)]
-        chain(1, whole, 1)
-        add_centre(0, best01, halves[0])
-        chain(1, whole, 2)
-        chain(0, halves[0], 1)
-        chain(1, whole, 3)
-        chain(0, halves[0], 2)
+        larger(partial3, picked[3][:, 0], picked[3][:, 1])
+        larger(best01, pairs[:, :, 0], pairs[:, :, 1])
+        larger(partial3, partial3, picked[3][:, 2])
+        add_centre(0, best01[:, :, halves[0]], halves[0])
+        chain(halves[0], 1)
+        larger(picked[0][:, 3], partial3, picked[3][:, 3])
+        chain(halves[0], 2)
+        add_centre(0, best01[:, :, halves[1]], halves[1])
+        chain(halves[0], 3)
         quantize(w3_mx)
-        chain(0, halves[0], 3)
-        add_centre(0, best01, halves[1])
-        add_centre(1, best23, halves[0])
-        chain(0, halves[1], 1)
+        add_centre(1, late_best(halves[0]), halves[0])
+        chain(halves[1], 1)
         relu_weave(z_mx[0], pieces[0])
-        chain(0, halves[1], 2)
+        chain(halves[1], 2)
         project_out(z_mx[0], pieces[0], banks[0], nc.scalar.copy, nc.sync.dma_start)
         for cols in pieces[1:]:
-            chain(0, cols, 3)
+            chain(cols, 3)
         for cols in pieces[1:]:
-            add_centre(1, best23, cols)
+            add_centre(1, late_best(cols), cols)
         relu_weave(z_mx[1], pieces[1])
         relu_weave(z_mx[2], pieces[2])
         project_out(z_mx[1], pieces[1], banks[1], nc.vector.tensor_copy, nc.sync.dma_start)

@@ -195,7 +195,7 @@ def tile_picked_wedgecv_relu_l_kernel(
         partial3 = maxima[:, 4]
         rows = early[:].rearrange("p t d (h v) -> p (t d h) v", h=2)
         best01 = picked[0][:, :2]
-        best23 = (rows[:, 4:7:2], rows[:, 14:6:-7])
+        best23 = (rows[:, 4:7:2], rows[:, 3:8:4])
 
         larger(pairs, early[:, :, :2], early[:, :, 2:])
         pieces = (halves[0], slice(HALF, HALF + P), slice(HALF + P, T))
@@ -222,16 +222,16 @@ def tile_picked_wedgecv_relu_l_kernel(
         chain(halves[0], 1)
         larger(picked[0][:, 3], partial3, picked[3][:, 3])
         chain(halves[0], 2)
+        quantize(w3_mx)
         add_centre(0, best01[:, :, halves[1]], halves[1])
         chain(halves[0], 3)
-        quantize(w3_mx)
-        add_centre(1, late_best(halves[0]), halves[0])
         chain(halves[1], 1)
-        relu_weave(z_mx[0], pieces[0])
+        add_centre(1, late_best(halves[0]), halves[0])
         chain(halves[1], 2)
-        project_out(z_mx[0], pieces[0], banks[0], nc.scalar.copy, nc.sync.dma_start)
+        relu_weave(z_mx[0], pieces[0])
         for cols in pieces[1:]:
             chain(cols, 3)
+        project_out(z_mx[0], pieces[0], banks[0], nc.scalar.copy, nc.sync.dma_start)
         for cols in pieces[1:]:
             add_centre(1, late_best(cols), cols)
         relu_weave(z_mx[1], pieces[1])

@@ -122,12 +122,13 @@ def tile_picked_wedgecv_relu_l_kernel(
         for bank, cols, copy in zip((banks[0], banks[7]), halves, (nc.vector.tensor_copy, nc.scalar.copy)):
             project(w2_mx[0], 0, bank[:, :HALF], cols)
             copy(windows[0][:, cols], bank[:, :HALF])
-        for bank, cols in zip((banks[1], banks[6]), halves):
+        for bank, cols, copy in zip((banks[1], banks[6]), halves, (nc.vector.tensor_copy, nc.scalar.copy)):
             project(w2_mx[1], 0, bank[:, :HALF], cols)
-            nc.scalar.copy(windows[1][:, cols], bank[:, :HALF])
-        for t, tiles, first_col in ((3, w2_mx[2], P), (2, w2_mx[2], 0)):
-            project(tiles, first_col, banks[t][:], whole)
-            nc.scalar.copy(windows[t][:, :T], banks[t][:])
+            copy(windows[1][:, cols], bank[:, :HALF])
+        for bank, cols in zip((banks[3], banks[5]), halves):
+            project(w2_mx[2], P, bank[:, :HALF], cols)
+            nc.scalar.copy(windows[3][:, cols], bank[:, :HALF])
+        project(w2_mx[2], 0, banks[2][:], whole)
 
         w1_mx = mx_tiles("w1", H)
         for t in range(PACK):
@@ -144,9 +145,11 @@ def tile_picked_wedgecv_relu_l_kernel(
         def fetch(t, d, cols):
             nc.scalar.activation(picked[t][:, d, cols], looked_up(t, d, cols), COPY)
 
-        for t, d in [(0, 0), (1, 0), (0, 1), (0, 2), (0, 3)]:
+        for t, d in [(0, 0), (0, 1), (0, 2), (0, 3), (1, 3)]:
             nc.vector.tensor_copy(picked[t][:, d, :], looked_up(t, d, whole))
-        for t, d in [(1, d) for d in range(1, 4)] + [(3, d) for d in range(4)]:
+        fetch(1, 0, whole)
+        nc.scalar.copy(windows[2][:, :T], banks[2][:])
+        for t, d in [(1, 1), (1, 2)] + [(3, d) for d in range(4)]:
             fetch(t, d, whole)
 
         quantize(w1_mx)

@@ -122,7 +122,7 @@ def tile_picked_wedgecv_relu_l_kernel(
         for bank, cols, copy in zip((banks[0], banks[7]), halves, (nc.vector.tensor_copy, nc.scalar.copy)):
             project(w2_mx[0], 0, bank[:, :HALF], cols)
             copy(windows[0][:, cols], bank[:, :HALF])
-        for bank, cols, copy in zip((banks[1], banks[6]), halves, (nc.vector.tensor_copy, nc.scalar.copy)):
+        for bank, cols, copy in zip((banks[1], banks[6]), halves, (nc.scalar.copy, nc.scalar.copy)):
             project(w2_mx[1], 0, bank[:, :HALF], cols)
             copy(windows[1][:, cols], bank[:, :HALF])
         for bank, cols in zip((banks[3], banks[5]), halves):

@@ -196,22 +196,18 @@ def tile_picked_wedgecv_relu_l_kernel(
         maxima = keep.tile([P, 5, T], F32, name="maxima", tag="w3_raw")
         pairs = maxima[:, :4].rearrange("p (t k) v -> p t k v", k=2)
         partial3 = maxima[:, 4]
-        rows = early[:].rearrange("p t d (h v) -> p (t d h) v", h=2)
         best01 = picked[0][:, :2]
-        best23 = (rows[:, 4:7:2], rows[:, 3:8:4])
+        best23 = picked[0][:, 2:]
 
         larger(pairs, early[:, :, :2], early[:, :, 2:])
         pieces = (halves[0], slice(HALF, HALF + P), slice(HALF + P, T))
-        for d in range(4):
-            fetch(2, d, halves[0])
-        for d in range(3):
-            fetch(2, d, halves[1])
+        for d, cols in ((0, whole), (1, whole), (2, halves[0]), (3, halves[0]), (2, halves[1])):
+            fetch(2, d, cols)
         for cols in pieces[1:]:
             fetch(2, 3, cols)
 
         def late_best(cols):
-            h, first = divmod(cols.start, HALF)
-            return best23[h][:, :, first : first + cols.stop - cols.start]
+            return best23[:, :, cols]
 
         def chain(cols, d):
             best = late_best(cols)[:, 0]
@@ -222,21 +218,21 @@ def tile_picked_wedgecv_relu_l_kernel(
         larger(best01, pairs[:, :, 0], pairs[:, :, 1])
         larger(partial3, partial3, picked[3][:, 2])
         add_centre(0, best01[:, :, halves[0]], halves[0])
-        chain(halves[0], 1)
         larger(picked[0][:, 3], partial3, picked[3][:, 3])
-        chain(halves[0], 2)
+        for cols in halves:
+            chain(cols, 1)
         quantize(w3_mx)
+        chain(halves[0], 2)
         add_centre(0, best01[:, :, halves[1]], halves[1])
         chain(halves[0], 3)
-        chain(halves[1], 1)
-        add_centre(1, late_best(halves[0]), halves[0])
         chain(halves[1], 2)
-        relu_weave(z_mx[0], pieces[0])
+        add_centre(1, late_best(halves[0]), halves[0])
         for cols in pieces[1:]:
             chain(cols, 3)
-        project_out(z_mx[0], pieces[0], banks[0], nc.scalar.copy, nc.sync.dma_start)
+        relu_weave(z_mx[0], pieces[0])
         for cols in pieces[1:]:
             add_centre(1, late_best(cols), cols)
+        project_out(z_mx[0], pieces[0], banks[0], nc.scalar.copy, nc.sync.dma_start)
         relu_weave(z_mx[1], pieces[1])
         relu_weave(z_mx[2], pieces[2])
         project_out(z_mx[1], pieces[1], banks[1], nc.vector.tensor_copy, nc.sync.dma_start)

from contextlib import ExitStack

import concourse.mybir as mybir

K, T, H, N = 512, 512, 512, 128
FLOPS = 2 * K * H * T * 2 + 2 * H * N * T

F32 = mybir.dt.float32
BF16 = mybir.dt.bfloat16
I32 = mybir.dt.int32
U32 = mybir.dt.uint32
U16 = mybir.dt.uint16
U8 = mybir.dt.uint8
FP8X4 = mybir.dt.float8_e4m3fn_x4
FP4X4 = mybir.dt.float4_e2m1fn_x4
COPY = mybir.ActivationFunctionType.Copy
MULT = mybir.AluOpType.mult
ADD = mybir.AluOpType.add
MAX = mybir.AluOpType.max

P = 128
PACK = 4
LIST_ROWS = 16
VECTOR_WINDOW = 704
SCALAR_WINDOW = T + LIST_ROWS
HALF = T // 2


def tile_picked_wedgecv_relu_l_kernel(
    tc, x_words, x_scales, w1, w2, w3, pos1, pos2, pos3, pos4, out
):
    nc = tc.nc
    with ExitStack() as ctx:
        lists = ctx.enter_context(tc.tile_pool(name="lists", bufs=1))
        keep = ctx.enter_context(tc.tile_pool(name="keep", bufs=1))
        psum = ctx.enter_context(tc.psum_pool(name="psum", bufs=1))

        x_codes = keep.tile([P, 2 * T], U8, name="x_codes", align_bytes=64)
        x_plane = keep.tile([P, T], U8, name="x_plane", align_bytes=64)
        nc.vector.memset(x_plane[:].bitcast(I32), 0)

        w2_rows = w2.rearrange("(p j) c -> p j c", j=PACK)
        w2_raw = [keep.tile([P, 2, H], F32, name="w2_raw%d" % h) for h in range(2)]
        for h in range(2):
            nc.sync.dma_start(w2_raw[h][:], w2_rows[:, 2 * h : 2 * h + 2])
        for q in range(4):
            nc.sync.dma_start(
                x_plane[32 * q : 32 * q + 4, :].bitcast(I32), x_scales[0, 4 * q : 4 * q + 4, :].bitcast(I32)
            )
        nc.sync.dma_start(x_codes[:].bitcast(I32), x_words[0].bitcast(I32))
        offsets = [lists.tile([P, T // LIST_ROWS], U16, name="offsets%d" % d) for d in range(4)]
        nc.sync.dma_start(offsets[0][:], pos1)
        w1_rows = keep.tile([P, PACK, H], F32, name="w1_rows", tag="w1_rows", align_bytes=64)
        w1_raw = w1_rows[:]
        nc.sync.dma_start(w1_raw, w1.rearrange("(p j) c -> p j c", j=PACK))
        for tile, pos in zip(offsets[1:], (pos2, pos3, pos4)):
            nc.sync.dma_start(tile[:], pos)
        w3_raw = keep.tile([P, PACK, N], F32, name="w3_raw", tag="w3_raw")
        w3_rows = w3.rearrange("(q t r) n -> t q r n", t=PACK, r=8)
        for t in range(PACK):
            nc.sync.dma_start(w3_raw[:, t, :], w3_rows[t])

        windows = [
            keep.tile([P, SCALAR_WINDOW if t > 1 else VECTOR_WINDOW], F32, name="window%d" % t) for t in range(PACK)
        ]
        for t in range(2):
            nc.vector.memset(windows[t][:, T:], 0.0)
        for t in range(2, PACK):
            nc.scalar.activation(windows[t][:, T:], windows[0][:, T:SCALAR_WINDOW], COPY)

        def mx_tiles(name, columns, slot=None):
            return (
                keep.tile([P, columns, PACK], BF16, name=name + "_bf", tag=name + "_bf", align_bytes=64),
                keep.tile([P, columns], U32, name=name + "_codes", tag=slot or name + "_codes", align_bytes=64),
                keep.tile([P, columns], U8, name=name + "_plane", align_bytes=64),
            )

        def quantize(tiles, cols=slice(None)):
            nc.vector.quantize_mx(
                tiles[1][:, cols].bitcast(FP8X4), tiles[2][:, cols], tiles[0][:, cols].rearrange("p m j -> p (m j)")
            )

        def layer_views(raw, rounded, t):
            return (
                rounded.rearrange("p (q r) j -> p q r j", r=8),
                raw.rearrange("p j (q t r) -> p t q r j", t=PACK, r=8)[:, t],
            )

        banks = [psum.tile([P, T], F32, name="bank%d" % b) for b in range(8)]

        def project(tiles, first_col, dst, cols):
            layer = slice(first_col, first_col + P)
            nc.tensor.matmul_mx(
                dst,
                tiles[1][:, layer].bitcast(FP8X4),
                tiles[2][:, layer],
                x_codes[:, 2 * cols.start : 2 * cols.stop].bitcast(FP4X4),
                x_plane[:, cols],
                start=True,
                stop=True,
            )

        whole = slice(0, T)
        halves = (slice(0, HALF), slice(HALF, T))
        groups = ((0, 1), (1, 2), (2, 4))
        w2_mx = [mx_tiles("w2_%d" % first, (last - first) * P) for first, last in groups]

        def deal(copy, h, g, blocks=slice(0, 16)):
            first, last = groups[g]
            dealt = w2_mx[g][0][:, :, 2 * h : 2 * h + 2].rearrange("p (t q r) j -> p q t r j", q=16, r=8)
            raw = w2_raw[h][:].rearrange("p j (q t r) -> p q t r j", t=PACK, r=8)[:, :, first:last]
            copy(dealt[:, blocks], raw[:, blocks])

        for g, copy in enumerate((nc.vector.tensor_copy, nc.vector.tensor_copy, nc.scalar.copy)):
            deal(copy, 0, g)
        deal(nc.vector.tensor_copy, 1, 0, slice(0, 8))
        deal(nc.scalar.copy, 1, 0, slice(8, 16))
        deal(nc.vector.tensor_copy, 1, 1)
        deal(nc.scalar.copy, 1, 2)
        for tiles in w2_mx:
            quantize(tiles)
        for bank, cols, copy in zip((banks[0], banks[7]), halves, (nc.vector.tensor_copy, nc.scalar.copy)):
            project(w2_mx[0], 0, bank[:, :HALF], cols)
            copy(windows[0][:, cols], bank[:, :HALF])
        for bank, cols, copy in zip((banks[1], banks[6]), halves, (nc.scalar.copy, nc.scalar.copy)):
            project(w2_mx[1], 0, bank[:, :HALF], cols)
            copy(windows[1][:, cols], bank[:, :HALF])
        for bank, cols in zip((banks[3], banks[5]), halves):
            project(w2_mx[2], P, bank[:, :HALF], cols)
            nc.scalar.copy(windows[3][:, cols], bank[:, :HALF])
        project(w2_mx[2], 0, banks[2][:], whole)

        w1_mx = mx_tiles("w1", H)
        for t in range(PACK):
            nc.gpsimd.tensor_scalar(*layer_views(w1_raw, w1_mx[0][:, t * P : (t + 1) * P, :], t), 1.0, 0.0, MULT, ADD)
        w3_mx = mx_tiles("w3", N, "w1_rows")
        nc.gpsimd.tensor_scalar(w3_mx[0][:], w3_raw[:].rearrange("p j n -> p n j"), 1.0, 0.0, MULT, ADD)

        early = keep.tile([P, 2, 4, T], F32, name="early")
        picked = [early[:, 0], early[:, 1], early[:, 1], w1_raw]

        def looked_up(t, d, cols):
            return windows[t][:].indirect(offsets[d][:, cols.start // LIST_ROWS : cols.stop // LIST_ROWS])

        def fetch(t, d, cols):
            nc.scalar.activation(picked[t][:, d, cols], looked_up(t, d, cols), COPY)

        for t, d in [(0, 0), (0, 1), (0, 2), (0, 3), (1, 3)]:
            nc.vector.tensor_copy(picked[t][:, d, :], looked_up(t, d, whole))
        fetch(1, 0, whole)
        nc.scalar.copy(windows[2][:, :T], banks[2][:])
        for t, d in [(1, 1), (1, 2)] + [(3, d) for d in range(4)]:
            fetch(t, d, whole)

        quantize(w1_mx)
        for u in range(2):
            for h in range(2):
                for e in range(2):
                    project(w1_mx, (2 * u + e) * P, banks[4 + 2 * u + h][:, e * HALF : (e + 1) * HALF], halves[h])

        edges = keep.tile([P, 2, T, 2], BF16, name="edges")

        def larger(dst, a, b):
            nc.vector.tensor_tensor(dst, a, b, MAX)

        def add_centre(u, best, cols):
            h, first = divmod(cols.start, HALF)
            centre = banks[4 + 2 * u + h][:].rearrange("p (e v) -> p v e", e=2)[:, first : first + cols.stop - cols.start]
            nc.vector.tensor_tensor(edges[:, u, cols], centre, best.rearrange("p e v -> p v e"), ADD)

        def relu_weave(tiles, cols):
            nc.vector.tensor_scalar(
                tiles[0][:].rearrange("p v (u e) -> p v u e", u=2),
                edges[:, :, cols].rearrange("p u v e -> p v u e"),
                0.0,
                None,
                MAX,
            )

        def project_out(tiles, cols, bank, copy, store):
            count = cols.stop - cols.start
            result = keep.tile([P, count], F32, name="result%d" % cols.start)
            quantize(tiles)
            nc.tensor.matmul_mx(
                bank[:, :count],
                w3_mx[1][:].bitcast(FP8X4),
                w3_mx[2][:],
                tiles[1][:].bitcast(FP8X4),
                tiles[2][:],
                start=True,
                stop=True,
            )
            copy(result[:], bank[:, :count])
            store(out[:, cols], result[:])

        maxima = keep.tile([P, 5, T], F32, name="maxima", tag="w3_raw")
        pairs = maxima[:, :4].rearrange("p (t k) v -> p t k v", k=2)
        partial3 = maxima[:, 4]
        best01 = picked[0][:, :2]
        best23 = picked[0][:, 2:]

        larger(pairs, early[:, :, :2], early[:, :, 2:])
        pieces = (halves[0], slice(HALF, HALF + P), slice(HALF + P, T))
        for d, cols in ((0, whole), (1, whole), (2, halves[0]), (3, halves[0]), (2, halves[1])):
            fetch(2, d, cols)
        for cols in pieces[1:]:
            fetch(2, 3, cols)

        def late_best(cols):
            return best23[:, :, cols]

        def chain(cols, d):
            best = late_best(cols)[:, 0]
            larger(best, best if d > 1 else picked[2][:, 0, cols], picked[2][:, d, cols])

        z_mx = [mx_tiles("z%d" % i, cols.stop - cols.start) for i, cols in enumerate(pieces)]
        larger(partial3, picked[3][:, 0], picked[3][:, 1])
        larger(best01, pairs[:, :, 0], pairs[:, :, 1])
        larger(partial3, partial3, picked[3][:, 2])
        add_centre(0, best01[:, :, halves[0]], halves[0])
        larger(picked[0][:, 3], partial3, picked[3][:, 3])
        for cols in halves:
            chain(cols, 1)
        quantize(w3_mx)
        chain(halves[0], 2)
        add_centre(0, best01[:, :, halves[1]], halves[1])
        chain(halves[0], 3)
        chain(halves[1], 2)
        add_centre(1, late_best(halves[0]), halves[0])
        for cols in pieces[1:]:
            chain(cols, 3)
        relu_weave(z_mx[0], pieces[0])
        for cols in pieces[1:]:
            add_centre(1, late_best(cols), cols)
        project_out(z_mx[0], pieces[0], banks[0], nc.scalar.copy, nc.sync.dma_start)
        relu_weave(z_mx[1], pieces[1])
        relu_weave(z_mx[2], pieces[2])
        project_out(z_mx[1], pieces[1], banks[1], nc.vector.tensor_copy, nc.sync.dma_start)
        project_out(z_mx[2], pieces[2], banks[2], nc.scalar.copy, nc.scalar.dma_start)
